import numpy as np
import ml_dtypes


def mxq(x, axis, fmt="e4m3"):
    dtype, down = {"e4m3": (ml_dtypes.float8_e4m3fn, 7), "e5m2": (ml_dtypes.float8_e5m2, 14)}[fmt]
    v = np.moveaxis(np.asarray(x, np.float32).astype(ml_dtypes.bfloat16).astype(np.float64), axis, -1)
    blocks = v.reshape(v.shape[:-1] + (-1, 32))
    amax = np.abs(blocks).max(-1, keepdims=True)
    byte = np.maximum(np.where(amax > 0, np.frexp(amax)[1] - 1 + 127, 0) - down, 1)
    scale = np.exp2(byte - 127.0)
    codes = (blocks / scale).astype(np.float32).astype(dtype).astype(np.float64)
    return np.moveaxis((codes * scale).reshape(v.shape), -1, axis)


WIDE = False


def mx_kscale(k):
    if not WIDE:
        return np.ones(k)
    levels = np.array([24, -24, 12, -12, 0])
    if k % 512:
        return np.exp2(np.random.permutation(np.resize(levels, k // 32))).repeat(32)
    a = np.empty((k // 512, 16))
    for p in range(k // 512):
        a[p, :8] = np.random.permutation(np.resize(levels, 8))
        for g in range(8):
            far = levels[np.abs(levels - a[p, g]) >= 10]
            a[p, g + 8] = far[np.random.randint(len(far))]
    return np.exp2(a.ravel()).repeat(32)


def f64(x):
    return np.asarray(x).astype(np.float64)


def striped8(idx):
    return np.concatenate([v.reshape(-1, 16).T for v in idx]).astype(np.uint16)


def unstriped8(offs):
    return np.stack([offs[16 * g:16 * g + 16].T.reshape(-1) for g in range(8)]).astype(np.int64)


def planes(y):
    n, m = y.shape
    v = y.astype(np.float32).astype(ml_dtypes.bfloat16).astype(np.float64).reshape(n // 32, 32, m)
    top = np.abs(v).max(1)
    byte = np.clip(np.where(top > 0, np.frexp(top)[1] - 1 + 127 - 7, 1), 1, 254)
    codes = (v * np.exp2(127.0 - byte)[:, None, :]).reshape(n, m).astype(np.float32).astype(ml_dtypes.float8_e4m3fn).view(np.uint8)
    words = codes.reshape(n // 512, 128, 4, m).transpose(0, 1, 3, 2)
    return np.ascontiguousarray(words), np.ascontiguousarray(byte.astype(np.uint8).reshape(n // 512, 16, m))


def silu(f):
    return f / (1.0 + np.exp(-np.maximum(f, -700.0)))


K, L, N, T, J = 512, 512, 512, 2048, 1024


def setup_inputs():
    n = np.random.standard_normal
    s = mx_kscale(K)[:, None]
    return {
        "xT": (n((K, T)) * s).astype(np.float32),
        "wgt": np.repeat(np.random.uniform(0.5, 2.0, (8, J)), 16, axis=0).astype(np.float32),
        "wt": (n((K, N)) / np.sqrt(K) / s).astype(np.float32),
        "b": (0.3 * n(N)).astype(np.float32),
        "offs": striped8(np.stack([np.random.permutation(T)[:J] for _ in range(8)])),
    }


def reference(xT, wgt, wt, b, offs):
    idx = unstriped8(offs)
    rows = np.arange(K)
    xg = f64(wgt)[rows // 4 % 128] * f64(xT)[rows[:, None], idx[rows % 512 // 64]]
    xT_ = mxq(xg, 0, "e4m3")
    wt_q_ = mxq(f64(wt), 0, "e4m3")
    wt_r_ = mxq(f64(wt) - wt_q_, 0, "e4m3")
    y = wt_q_.T @ xT_ + wt_r_.T @ xT_
    out_0 = silu(y + f64(b)[:, None])
    return (out_0,) + planes(out_0)

@@ -1,0 +1,199 @@
+from contextlib import ExitStack
+
+import concourse.mybir as mybir
+from concourse.masks import make_identity
+
+K, N, T, J = 512, 512, 2048, 1024
+FLOPS = 2 * 2 * K * N * J + 2 * K * K * N
+
+F32 = mybir.dt.float32
+BF16 = mybir.dt.bfloat16
+I32 = mybir.dt.int32
+U32 = mybir.dt.uint32
+U16 = mybir.dt.uint16
+U8 = mybir.dt.uint8
+FP8X4 = mybir.dt.float8_e4m3fn_x4
+MULT = mybir.AluOpType.mult
+SUBTRACT = mybir.AluOpType.subtract
+SILU = mybir.ActivationFunctionType.Silu
+
+P = 128
+PACK = 4
+CHUNKS = (256, 256, 256, 128, 128)
+
+
+def tile_list_tier_no_siluP_kernel(tc, xT, wgt, wt, b, offs, out_0, out_1, out_2):
+    nc = tc.nc
+    with ExitStack() as ctx:
+        lists = ctx.enter_context(tc.tile_pool(name="lists", bufs=1))
+        keep = ctx.enter_context(tc.tile_pool(name="keep", bufs=1))
+        reuse = ctx.enter_context(tc.tile_pool(name="reuse", bufs=1))
+        psum = ctx.enter_context(tc.psum_pool(name="psum", bufs=8))
+
+        def sbuf(shape, dtype, name, tag=None):
+            return keep.tile(shape, dtype, name=name, tag=tag or name, align_bytes=64)
+
+        starts = [sum(CHUNKS[:c]) for c in range(len(CHUNKS))]
+        half = J // 2
+
+        offsets = lists.tile([P, J // 16], U16, name="offsets")
+        wt_rows = wt.rearrange("(p i) n -> p i n", i=PACK)
+        x_rows = xT.rearrange("(p i) t -> p i t", i=PACK)
+        w_raw = [reuse.tile([P, PACK, N // 2], F32, name="w_raw%d" % h, offset=4096 * h) for h in range(2)]
+        x_plane = [sbuf([P, T], F32, "x_plane%d" % i) for i in range(PACK)]
+        gate = [sbuf([P, half], F32, "gate%d" % h) for h in range(2)]
+        bias = sbuf([P, PACK], F32, "bias")
+        for h in range(2):
+            nc.sync.dma_start(out=w_raw[h][:], in_=wt_rows[:, :, h * (N // 2) : (h + 1) * (N // 2)])
+        nc.sync.dma_start(offsets[:], offs)
+        nc.sync.dma_start(out=x_plane[0][:], in_=x_rows[:, 0, :])
+        for h in range(2):
+            nc.sync.dma_start(out=gate[h][:], in_=wgt[:, h * half : (h + 1) * half])
+        for i in range(1, PACK):
+            nc.sync.dma_start(out=x_plane[i][:], in_=x_rows[:, i, :])
+        nc.sync.dma_start(out=bias[:], in_=b.rearrange("(p t) -> p t", t=PACK))
+
+        warm = sbuf([P, 1], F32, "warm")
+        nc.vector.memset(warm[:], 0.0)
+        warm_out = sbuf([P, 1], F32, "warm_out")
+        nc.scalar.activation(out=warm_out[:], in_=warm[:], func=SILU)
+
+        eye = sbuf([P, P], BF16, "eye")
+        make_identity(nc, eye[:])
+        eye_grouped = reuse.tile([P, PACK * (K + 1)], BF16, name="eye_grouped", offset=10240, align_bytes=64)
+        nc.vector.memset(eye_grouped[:].bitcast(I32), 0)
+        nc.vector.tensor_copy(out=eye_grouped[:].rearrange("p (i r) -> p i r", i=PACK)[:, :, 0:K:PACK],
+                              in_=eye[:].unsqueeze(1).to_broadcast([P, PACK, P]))
+        eye_codes = sbuf([P, K], U32, "eye_codes")
+        eye_scales = sbuf([P, K], U8, "eye_scales")
+        nc.vector.quantize_mx(out=eye_codes[:].bitcast(FP8X4), scales=eye_scales[:],
+                              in_=eye_grouped[:, 0 : PACK * K])
+
+        rest_grouped = sbuf([P, PACK, P, PACK], BF16, "rest_grouped")
+        main_grouped = sbuf([P, PACK, P, PACK], BF16, "main_grouped")
+        plains = []
+        rests = []
+        for q in range(4):
+            raw = w_raw[q // 2][:, :, (q % 2) * P : (q % 2 + 1) * P]
+            plain = reuse.tile([P, P, PACK], BF16, name="plain%d" % q, offset=10240 + 1024 * q, align_bytes=64)
+            nc.scalar.copy(out=plain[:].rearrange("p (c e) i -> p c i e", e=2),
+                           in_=raw.rearrange("p i (c e) -> p c i e", e=2))
+            plains.append(plain)
+            codes = sbuf([P, P], U32, "plain_codes%d" % q)
+            scales = sbuf([P, P], U8, "plain_scales%d" % q)
+            nc.vector.quantize_mx(out=codes[:].bitcast(FP8X4), scales=scales[:],
+                                  in_=plain[:].rearrange("p n i -> p (n i)"))
+            values = psum.tile([P, PACK, P], F32, name="values", tag="bank")
+            for i in range(PACK):
+                nc.tensor.matmul_mx(out=values[:, i, :], lhsT=eye_codes[:, i * P : (i + 1) * P].bitcast(FP8X4),
+                                    lhsT_scale=eye_scales[:, i * P : (i + 1) * P],
+                                    rhs=codes[:].bitcast(FP8X4), rhs_scale=scales[:], start=True, stop=True)
+            rest = sbuf([P, P, PACK], BF16, "rest%d" % q)
+            rests.append(rest)
+            nc.vector.tensor_tensor(
+                out=rest[:].rearrange("p (c e) i -> p c i e", e=2),
+                in0=raw.rearrange("p i (c e) -> p c i e", e=2),
+                in1=values[:].rearrange("p i (c e) -> p c i e", e=2),
+                op=SUBTRACT)
+        for grouped, quarters in ((main_grouped, plains), (rest_grouped, rests)):
+            dealt = grouped[:].rearrange("p t m i -> p (t m i)").bitcast(F32).rearrange("p (t m e) -> p m t e", t=PACK, e=2)
+            for q in range(4):
+                nc.scalar.copy(out=dealt[:, 32 * q : 32 * (q + 1)],
+                               in_=quarters[q][:].rearrange("p n i -> p (n i)").bitcast(F32).rearrange("p (m t e) -> p m t e", t=PACK, e=2))
+        tiers = []
+        for name, grouped in (("main", main_grouped), ("rest", rest_grouped)):
+            codes = sbuf([P, N], U32, name + "_codes")
+            scales = sbuf([P, N], U8, name + "_scales")
+            nc.vector.quantize_mx(out=codes[:].bitcast(FP8X4), scales=scales[:],
+                                  in_=grouped[:].rearrange("p t m i -> p (t m i)"))
+            tiers.append((codes, scales))
+
+        def gather(dst, i, j0, width):
+            h = j0 // half
+            nc.vector.tensor_tensor(out=dst, in0=x_plane[i][:].indirect(offsets[:, j0 // 16 : (j0 + width) // 16]),
+                                    in1=gate[h][:, j0 - h * half : j0 - h * half + width], op=MULT)
+
+        low = [reuse.tile([P, 2, half], F32, name="low%d" % h, offset=2048 + 4096 * h) for h in range(2)]
+        for i in range(2):
+            for h in range(2):
+                gather(low[h][:, i, :], i, h * half, half)
+        high = [sbuf([P, 2, CHUNKS[c]], F32, "high%d" % c, tag="x_plane%d" % (1 - c))[:] for c in range(2)]
+        xg = [sbuf([P, w, PACK], BF16, "xg%d" % c, tag="chunk%d" % c) for c, w in enumerate(CHUNKS)]
+
+        def weave_pair(engine_copy, c, pair, src):
+            engine_copy(out=xg[c][:, :, 2 * pair : 2 * pair + 2].rearrange("p (c e) i -> p c e i", e=4),
+                        in_=src.rearrange("p i (c e) -> p c e i", e=4))
+
+        def weave_low(c):
+            h = starts[c] // half
+            j = starts[c] - h * half
+            weave_pair(nc.scalar.copy, c, 0, low[h][:, :, j : j + CHUNKS[c]])
+
+        for c in range(len(CHUNKS)):
+            weave_low(c)
+        for c in range(2):
+            gather(high[c][:, 0, :], 2, starts[c], CHUNKS[c])
+
+        out_rows = out_0.rearrange("(p t) j -> p t j", t=PACK)
+        out_words = out_1.rearrange("a p j i -> p (a j i)").bitcast(I32)
+        out_scales = out_2.rearrange("a q j -> (a q) j").bitcast(I32)
+        y_scales = sbuf([P, J], U8, "y_scales")
+        xq = []
+        ys = []
+
+        def front(c):
+            w = CHUNKS[c]
+            if c >= 2:
+                high.append(sbuf([P, 2, w], F32, "high%d" % c, tag="chunk%d" % (c - 2))[:])
+                gather(high[c][:, 0, :], 2, starts[c], w)
+            gather(high[c][:, 1, :], 3, starts[c], w)
+            weave_pair(nc.scalar.copy, c, 1, high[c])
+
+        def quant_x(c):
+            w = CHUNKS[c]
+            codes = sbuf([P, w], U32, "xg_codes%d" % c)
+            scales = sbuf([P, w], U8, "xg_scales%d" % c)
+            nc.vector.quantize_mx(out=codes[:].bitcast(FP8X4), scales=scales[:], in_=xg[c][:].rearrange("p j i -> p (j i)"))
+            xq.append((codes, scales))
+
+        def multiply(c):
+            w = CHUNKS[c]
+            codes, scales = xq[c]
+            y = sbuf([P, PACK, w], F32, "y%d" % c)
+            for t in range(PACK):
+                acc = psum.tile([P, w], F32, name="acc", tag="bank")
+                for n, (w_codes, w_scales) in enumerate(tiers):
+                    nc.tensor.matmul_mx(out=acc[:], lhsT=w_codes[:, t * P : (t + 1) * P].bitcast(FP8X4),
+                                        lhsT_scale=w_scales[:, t * P : (t + 1) * P],
+                                        rhs=codes[:].bitcast(FP8X4), rhs_scale=scales[:], start=(n == 0), stop=(n == 1))
+                nc.scalar.activation(out=y[:, t, :], in_=acc[:], func=SILU, bias=bias[:, t : t + 1])
+                if t % 2 == 1:
+                    nc.sync.dma_start(out=out_rows[:, t - 1 : t + 1, starts[c] : starts[c] + w], in_=y[:, t - 1 : t + 1, :])
+            ys.append(y)
+
+        def planes(c):
+            w = CHUNKS[c]
+            grouped = sbuf([P, w, PACK], BF16, "y_grouped%d" % c)
+            nc.vector.tensor_copy(out=grouped[:].rearrange("p (c e) t -> p c t e", e=2),
+                                  in_=ys[c][:].rearrange("p t (c e) -> p c t e", e=2))
+            codes = sbuf([P, w], U32, "y_codes%d" % c)
+            nc.vector.quantize_mx(out=codes[:].bitcast(FP8X4), scales=y_scales[:, starts[c] : starts[c] + w],
+                                  in_=grouped[:].rearrange("p j t -> p (j t)"))
+            nc.sync.dma_start(out=out_words[:, starts[c] : starts[c] + w], in_=codes[:].bitcast(I32))
+
+        n_chunks = len(CHUNKS)
+        front(0)
+        front(1)
+        for step in range(n_chunks + 2):
+            if step < n_chunks:
+                quant_x(step)
+            if step + 2 < n_chunks:
+                front(step + 2)
+            if step < n_chunks:
+                multiply(step)
+            if 0 <= step - 2 < n_chunks:
+                planes(step - 2)
+        for quad in range(4):
+            queue = nc.sync if quad % 2 == 0 else nc.scalar
+            queue.dma_start(out=out_scales[4 * quad : 4 * quad + 4, :],
+                            in_=y_scales[32 * quad : 32 * quad + 4, :].bitcast(I32))

@@ -19,7 +19,9 @@ SILU = mybir.ActivationFunctionType.Silu
 
 P = 128
 PACK = 4
-CHUNKS = (256, 256, 256, 128, 128)
+CHUNKS = (128, 256, 256, 256, 128)
+STORE_GROUPS = ((0, 1), (2, 3), (4, 4))
+PARTS = ((0, 640), (640, 1024))
 
 
 def tile_list_tier_no_siluP_kernel(tc, xT, wgt, wt, b, offs, out_0, out_1, out_2):
@@ -34,22 +36,23 @@ def tile_list_tier_no_siluP_kernel(tc, xT, wgt, wt, b, offs, out_0, out_1, out_2
             return keep.tile(shape, dtype, name=name, tag=tag or name, align_bytes=64)
 
         starts = [sum(CHUNKS[:c]) for c in range(len(CHUNKS))]
-        half = J // 2
 
         offsets = lists.tile([P, J // 16], U16, name="offsets")
         wt_rows = wt.rearrange("(p i) n -> p i n", i=PACK)
         x_rows = xT.rearrange("(p i) t -> p i t", i=PACK)
-        w_raw = [reuse.tile([P, PACK, N // 2], F32, name="w_raw%d" % h, offset=4096 * h) for h in range(2)]
-        x_plane = [sbuf([P, T], F32, "x_plane%d" % i) for i in range(PACK)]
-        gate = [sbuf([P, half], F32, "gate%d" % h) for h in range(2)]
+        w_cols = ((0, 128), (128, 256), (256, 512))
+        w_raw = [reuse.tile([P, PACK, hi - lo], F32, name="w_raw%d" % lo, offset=16 * lo) for lo, hi in w_cols]
+        x_plane = [sbuf([P, T], F32, "x_plane%d" % i) for i in range(PACK - 1)]
+        x_plane.append(reuse.tile([P, T], F32, name="x_plane3", offset=16384, align_bytes=64))
+        gate = [sbuf([P, hi - lo], F32, "gate%d" % lo) for lo, hi in PARTS]
         bias = sbuf([P, PACK], F32, "bias")
-        for h in range(2):
-            nc.sync.dma_start(out=w_raw[h][:], in_=wt_rows[:, :, h * (N // 2) : (h + 1) * (N // 2)])
+        for piece, (lo, hi) in zip(w_raw, w_cols):
+            nc.sync.dma_start(out=piece[:], in_=wt_rows[:, :, lo:hi])
         nc.sync.dma_start(offsets[:], offs)
-        nc.sync.dma_start(out=x_plane[0][:], in_=x_rows[:, 0, :])
-        for h in range(2):
-            nc.sync.dma_start(out=gate[h][:], in_=wgt[:, h * half : (h + 1) * half])
-        for i in range(1, PACK):
+        for h, (lo, hi) in enumerate(PARTS):
+            nc.sync.dma_start(out=x_plane[h][:], in_=x_rows[:, h, :])
+            nc.sync.dma_start(out=gate[h][:], in_=wgt[:, lo:hi])
+        for i in range(2, PACK):
             nc.sync.dma_start(out=x_plane[i][:], in_=x_rows[:, i, :])
         nc.sync.dma_start(out=bias[:], in_=b.rearrange("(p t) -> p t", t=PACK))
 
@@ -60,7 +63,7 @@ def tile_list_tier_no_siluP_kernel(tc, xT, wgt, wt, b, offs, out_0, out_1, out_2
 
         eye = sbuf([P, P], BF16, "eye")
         make_identity(nc, eye[:])
-        eye_grouped = reuse.tile([P, PACK * (K + 1)], BF16, name="eye_grouped", offset=10240, align_bytes=64)
+        eye_grouped = reuse.tile([P, PACK * (K + 1)], BF16, name="eye_grouped", offset=11264, align_bytes=64)
         nc.vector.memset(eye_grouped[:].bitcast(I32), 0)
         nc.vector.tensor_copy(out=eye_grouped[:].rearrange("p (i r) -> p i r", i=PACK)[:, :, 0:K:PACK],
                               in_=eye[:].unsqueeze(1).to_broadcast([P, PACK, P]))
@@ -74,12 +77,16 @@ def tile_list_tier_no_siluP_kernel(tc, xT, wgt, wt, b, offs, out_0, out_1, out_2
         plains = []
         rests = []
         for q in range(4):
-            raw = w_raw[q // 2][:, :, (q % 2) * P : (q % 2 + 1) * P]
-            plain = reuse.tile([P, P, PACK], BF16, name="plain%d" % q, offset=10240 + 1024 * q, align_bytes=64)
-            nc.scalar.copy(out=plain[:].rearrange("p (c e) i -> p c i e", e=2),
+            raw = w_raw[q][:] if q < 2 else w_raw[2][:, :, (q - 2) * P : (q - 1) * P]
+            plain = reuse.tile([P, P, PACK], BF16, name="plain%d" % q, offset=11264 + 1024 * q, align_bytes=64)
+            round_copy = nc.vector.tensor_copy if q == 0 else nc.scalar.copy
+            round_copy(out=plain[:].rearrange("p (c e) i -> p c i e", e=2),
                            in_=raw.rearrange("p i (c e) -> p c i e", e=2))
             plains.append(plain)
-            codes = sbuf([P, P], U32, "plain_codes%d" % q)
+            if q == 3:
+                codes = reuse.tile([P, P], U32, name="plain_codes3", offset=2048, align_bytes=64)
+            else:
+                codes = sbuf([P, P], U32, "plain_codes%d" % q)
             scales = sbuf([P, P], U8, "plain_scales%d" % q)
             nc.vector.quantize_mx(out=codes[:].bitcast(FP8X4), scales=scales[:],
                                   in_=plain[:].rearrange("p n i -> p (n i)"))
@@ -109,14 +116,15 @@ def tile_list_tier_no_siluP_kernel(tc, xT, wgt, wt, b, offs, out_0, out_1, out_2
             tiers.append((codes, scales))
 
         def gather(dst, i, j0, width):
-            h = j0 // half
+            h = 0 if j0 < PARTS[1][0] else 1
+            j = j0 - PARTS[h][0]
             nc.vector.tensor_tensor(out=dst, in0=x_plane[i][:].indirect(offsets[:, j0 // 16 : (j0 + width) // 16]),
-                                    in1=gate[h][:, j0 - h * half : j0 - h * half + width], op=MULT)
+                                    in1=gate[h][:, j : j + width], op=MULT)
 
-        low = [reuse.tile([P, 2, half], F32, name="low%d" % h, offset=2048 + 4096 * h) for h in range(2)]
-        for i in range(2):
-            for h in range(2):
-                gather(low[h][:, i, :], i, h * half, half)
+        low = [reuse.tile([P, 2, hi - lo], F32, name="low%d" % lo, offset=2560 + 8 * lo) for lo, hi in PARTS]
+        for h, (lo, hi) in enumerate(PARTS):
+            for i in range(2):
+                gather(low[h][:, i, :], i, lo, hi - lo)
         high = [sbuf([P, 2, CHUNKS[c]], F32, "high%d" % c, tag="x_plane%d" % (1 - c))[:] for c in range(2)]
         xg = [sbuf([P, w, PACK], BF16, "xg%d" % c, tag="chunk%d" % c) for c, w in enumerate(CHUNKS)]
 
@@ -125,8 +133,8 @@ def tile_list_tier_no_siluP_kernel(tc, xT, wgt, wt, b, offs, out_0, out_1, out_2
                         in_=src.rearrange("p i (c e) -> p c e i", e=4))
 
         def weave_low(c):
-            h = starts[c] // half
-            j = starts[c] - h * half
+            h = 0 if starts[c] < PARTS[1][0] else 1
+            j = starts[c] - PARTS[h][0]
             weave_pair(nc.scalar.copy, c, 0, low[h][:, :, j : j + CHUNKS[c]])
 
         for c in range(len(CHUNKS)):
@@ -140,6 +148,7 @@ def tile_list_tier_no_siluP_kernel(tc, xT, wgt, wt, b, offs, out_0, out_1, out_2
         y_scales = sbuf([P, J], U8, "y_scales")
         xq = []
         ys = []
+        y_codes = []
 
         def front(c):
             w = CHUNKS[c]
@@ -173,26 +182,29 @@ def tile_list_tier_no_siluP_kernel(tc, xT, wgt, wt, b, offs, out_0, out_1, out_2
 
         def planes(c):
             w = CHUNKS[c]
-            grouped = sbuf([P, w, PACK], BF16, "y_grouped%d" % c)
+            grouped = reuse.tile([P, w, PACK], BF16, name="y_grouped%d" % c, offset=16384 + 8 * starts[c], align_bytes=64)
             nc.vector.tensor_copy(out=grouped[:].rearrange("p (c e) t -> p c t e", e=2),
                                   in_=ys[c][:].rearrange("p t (c e) -> p c t e", e=2))
-            codes = sbuf([P, w], U32, "y_codes%d" % c)
-            nc.vector.quantize_mx(out=codes[:].bitcast(FP8X4), scales=y_scales[:, starts[c] : starts[c] + w],
+            first, last = [group for group in STORE_GROUPS if group[0] <= c <= group[1]][0]
+            lo, hi = starts[first], starts[last] + CHUNKS[last]
+            if c == first:
+                y_codes.append(sbuf([P, hi - lo], U32, "y_codes%d" % c))
+            codes = y_codes[-1]
+            nc.vector.quantize_mx(out=codes[:, starts[c] - lo : starts[c] - lo + w].bitcast(FP8X4), scales=y_scales[:, starts[c] : starts[c] + w],
                                   in_=grouped[:].rearrange("p j t -> p (j t)"))
-            nc.sync.dma_start(out=out_words[:, starts[c] : starts[c] + w], in_=codes[:].bitcast(I32))
+            if c == last:
+                nc.sync.dma_start(out=out_words[:, lo:hi], in_=codes[:].bitcast(I32))
 
         n_chunks = len(CHUNKS)
         front(0)
         front(1)
-        for step in range(n_chunks + 2):
-            if step < n_chunks:
-                quant_x(step)
+        for step in range(n_chunks):
+            quant_x(step)
             if step + 2 < n_chunks:
                 front(step + 2)
-            if step < n_chunks:
-                multiply(step)
-            if 0 <= step - 2 < n_chunks:
-                planes(step - 2)
+            multiply(step)
+        for step in range(n_chunks):
+            planes(step)
         for quad in range(4):
             queue = nc.sync if quad % 2 == 0 else nc.scalar
             queue.dma_start(out=out_scales[4 * quad : 4 * quad + 4, :],

@@ -20,7 +20,7 @@ SILU = mybir.ActivationFunctionType.Silu
 P = 128
 PACK = 4
 CHUNKS = (128, 256, 256, 256, 128)
-STORE_GROUPS = ((0, 1), (2, 3), (4, 4))
+STORE_GROUPS = ((0, 1), (2, 2), (3, 3), (4, 4))
 PARTS = ((0, 640), (640, 1024))
 
 
@@ -41,19 +41,18 @@ def tile_list_tier_no_siluP_kernel(tc, xT, wgt, wt, b, offs, out_0, out_1, out_2
         wt_rows = wt.rearrange("(p i) n -> p i n", i=PACK)
         x_rows = xT.rearrange("(p i) t -> p i t", i=PACK)
         w_cols = ((0, 128), (128, 256), (256, 512))
-        w_raw = [reuse.tile([P, PACK, hi - lo], F32, name="w_raw%d" % lo, offset=16 * lo) for lo, hi in w_cols]
-        x_plane = [sbuf([P, T], F32, "x_plane%d" % i) for i in range(PACK - 1)]
-        x_plane.append(reuse.tile([P, T], F32, name="x_plane3", offset=16384, align_bytes=64))
+        w_raw = [reuse.tile([P, PACK, hi - lo], F32, name="w_raw%d" % lo, offset=4096 + 16 * lo) for lo, hi in w_cols]
+        x_plane = [sbuf([P, T], F32, "x_plane%d" % i) for i in range(PACK)]
         gate = [sbuf([P, hi - lo], F32, "gate%d" % lo) for lo, hi in PARTS]
         bias = sbuf([P, PACK], F32, "bias")
         for piece, (lo, hi) in zip(w_raw, w_cols):
             nc.sync.dma_start(out=piece[:], in_=wt_rows[:, :, lo:hi])
         nc.sync.dma_start(offsets[:], offs)
-        for h, (lo, hi) in enumerate(PARTS):
-            nc.sync.dma_start(out=x_plane[h][:], in_=x_rows[:, h, :])
-            nc.sync.dma_start(out=gate[h][:], in_=wgt[:, lo:hi])
-        for i in range(2, PACK):
+        nc.sync.dma_start(out=x_plane[0][:], in_=x_rows[:, 0, :])
+        nc.sync.dma_start(out=gate[0][:], in_=wgt[:, PARTS[0][0] : PARTS[0][1]])
+        for i in range(1, PACK):
             nc.sync.dma_start(out=x_plane[i][:], in_=x_rows[:, i, :])
+        nc.sync.dma_start(out=gate[1][:], in_=wgt[:, PARTS[1][0] : PARTS[1][1]])
         nc.sync.dma_start(out=bias[:], in_=b.rearrange("(p t) -> p t", t=PACK))
 
         warm = sbuf([P, 1], F32, "warm")
@@ -63,7 +62,7 @@ def tile_list_tier_no_siluP_kernel(tc, xT, wgt, wt, b, offs, out_0, out_1, out_2
 
         eye = sbuf([P, P], BF16, "eye")
         make_identity(nc, eye[:])
-        eye_grouped = reuse.tile([P, PACK * (K + 1)], BF16, name="eye_grouped", offset=11264, align_bytes=64)
+        eye_grouped = reuse.tile([P, PACK * (K + 1)], BF16, name="eye_grouped", offset=13440, align_bytes=64)
         nc.vector.memset(eye_grouped[:].bitcast(I32), 0)
         nc.vector.tensor_copy(out=eye_grouped[:].rearrange("p (i r) -> p i r", i=PACK)[:, :, 0:K:PACK],
                               in_=eye[:].unsqueeze(1).to_broadcast([P, PACK, P]))
@@ -78,13 +77,13 @@ def tile_list_tier_no_siluP_kernel(tc, xT, wgt, wt, b, offs, out_0, out_1, out_2
         rests = []
         for q in range(4):
             raw = w_raw[q][:] if q < 2 else w_raw[2][:, :, (q - 2) * P : (q - 1) * P]
-            plain = reuse.tile([P, P, PACK], BF16, name="plain%d" % q, offset=11264 + 1024 * q, align_bytes=64)
+            plain = reuse.tile([P, P, PACK], BF16, name="plain%d" % q, offset=13440 + 1024 * q, align_bytes=64)
             round_copy = nc.vector.tensor_copy if q == 0 else nc.scalar.copy
             round_copy(out=plain[:].rearrange("p (c e) i -> p c i e", e=2),
                            in_=raw.rearrange("p i (c e) -> p c i e", e=2))
             plains.append(plain)
             if q == 3:
-                codes = reuse.tile([P, P], U32, name="plain_codes3", offset=2048, align_bytes=64)
+                codes = reuse.tile([P, P], U32, name="plain_codes3", offset=6144, align_bytes=64)
             else:
                 codes = sbuf([P, P], U32, "plain_codes%d" % q)
             scales = sbuf([P, P], U8, "plain_scales%d" % q)
@@ -121,26 +120,26 @@ def tile_list_tier_no_siluP_kernel(tc, xT, wgt, wt, b, offs, out_0, out_1, out_2
             nc.vector.tensor_tensor(out=dst, in0=x_plane[i][:].indirect(offsets[:, j0 // 16 : (j0 + width) // 16]),
                                     in1=gate[h][:, j : j + width], op=MULT)
 
-        low = [reuse.tile([P, 2, hi - lo], F32, name="low%d" % lo, offset=2560 + 8 * lo) for lo, hi in PARTS]
-        for h, (lo, hi) in enumerate(PARTS):
-            for i in range(2):
-                gather(low[h][:, i, :], i, lo, hi - lo)
-        high = [sbuf([P, 2, CHUNKS[c]], F32, "high%d" % c, tag="x_plane%d" % (1 - c))[:] for c in range(2)]
-        xg = [sbuf([P, w, PACK], BF16, "xg%d" % c, tag="chunk%d" % c) for c, w in enumerate(CHUNKS)]
+        early = PARTS[0][1]
+        low = reuse.tile([P, 2, early], F32, name="low", offset=3136)
+        for i in range(2):
+            gather(low[:, i, :], i, 0, early)
+        high = [reuse.tile([P, 2, CHUNKS[c]], F32, name="high%d" % c, offset=8256 + 8 * starts[c]) for c in range(3)]
+        xg = [sbuf([P, CHUNKS[c], PACK], BF16, "xg%d" % c, tag="chunk%d" % c) for c in range(3)]
+        xg.append(reuse.tile([P, CHUNKS[3], PACK], BF16, name="xg3", offset=20480, align_bytes=64))
+        xg.append(sbuf([P, CHUNKS[4], PACK], BF16, "xg4"))
 
-        def weave_pair(engine_copy, c, pair, src):
-            engine_copy(out=xg[c][:, :, 2 * pair : 2 * pair + 2].rearrange("p (c e) i -> p c e i", e=4),
-                        in_=src.rearrange("p i (c e) -> p c e i", e=4))
+        def weave_pair(c, pair, src):
+            nc.scalar.copy(out=xg[c][:, :, 2 * pair : 2 * pair + 2].rearrange("p (c e) i -> p c e i", e=4),
+                           in_=src.rearrange("p i (c e) -> p c e i", e=4))
 
-        def weave_low(c):
-            h = 0 if starts[c] < PARTS[1][0] else 1
-            j = starts[c] - PARTS[h][0]
-            weave_pair(nc.scalar.copy, c, 0, low[h][:, :, j : j + CHUNKS[c]])
-
-        for c in range(len(CHUNKS)):
-            weave_low(c)
-        for c in range(2):
-            gather(high[c][:, 0, :], 2, starts[c], CHUNKS[c])
+        for c in range(3):
+            weave_pair(c, 0, low[:, :, starts[c] : starts[c] + CHUNKS[c]])
+        for i in range(2, PACK):
+            for c in range(3):
+                gather(high[c][:, i - 2, :], i, starts[c], CHUNKS[c])
+        for c in range(3):
+            weave_pair(c, 1, high[c][:])
 
         out_rows = out_0.rearrange("(p t) j -> p t j", t=PACK)
         out_words = out_1.rearrange("a p j i -> p (a j i)").bitcast(I32)
@@ -150,13 +149,17 @@ def tile_list_tier_no_siluP_kernel(tc, xT, wgt, wt, b, offs, out_0, out_1, out_2
         ys = []
         y_codes = []
 
-        def front(c):
+        picked = {}
+
+        def gather_all(c):
             w = CHUNKS[c]
-            if c >= 2:
-                high.append(sbuf([P, 2, w], F32, "high%d" % c, tag="chunk%d" % (c - 2))[:])
-                gather(high[c][:, 0, :], 2, starts[c], w)
-            gather(high[c][:, 1, :], 3, starts[c], w)
-            weave_pair(nc.scalar.copy, c, 1, high[c])
+            picked[c] = sbuf([P, PACK, w], F32, "picked%d" % c, tag="chunk%d" % (c - 2))
+            for i in range(PACK):
+                gather(picked[c][:, i, :], i, starts[c], w)
+
+        def weave_all(c):
+            nc.scalar.copy(out=xg[c][:].rearrange("p (c e) i -> p c i e", e=2),
+                           in_=picked[c][:].rearrange("p i (c e) -> p c i e", e=2))
 
         def quant_x(c):
             w = CHUNKS[c]
@@ -165,25 +168,31 @@ def tile_list_tier_no_siluP_kernel(tc, xT, wgt, wt, b, offs, out_0, out_1, out_2
             nc.vector.quantize_mx(out=codes[:].bitcast(FP8X4), scales=scales[:], in_=xg[c][:].rearrange("p j i -> p (j i)"))
             xq.append((codes, scales))
 
-        def multiply(c):
+        def multiply(c, slots):
             w = CHUNKS[c]
             codes, scales = xq[c]
-            y = sbuf([P, PACK, w], F32, "y%d" % c)
-            for t in range(PACK):
+            if slots[0] == 0:
+                ys.append(sbuf([P, PACK, w], F32, "y%d" % c))
+            y = ys[c]
+            for t in slots:
                 acc = psum.tile([P, w], F32, name="acc", tag="bank")
                 for n, (w_codes, w_scales) in enumerate(tiers):
                     nc.tensor.matmul_mx(out=acc[:], lhsT=w_codes[:, t * P : (t + 1) * P].bitcast(FP8X4),
                                         lhsT_scale=w_scales[:, t * P : (t + 1) * P],
                                         rhs=codes[:].bitcast(FP8X4), rhs_scale=scales[:], start=(n == 0), stop=(n == 1))
                 nc.scalar.activation(out=y[:, t, :], in_=acc[:], func=SILU, bias=bias[:, t : t + 1])
-                if t % 2 == 1:
-                    nc.sync.dma_start(out=out_rows[:, t - 1 : t + 1, starts[c] : starts[c] + w], in_=y[:, t - 1 : t + 1, :])
-            ys.append(y)
+                rows = 512 // w
+                if (t + 1) % rows == 0:
+                    nc.sync.dma_start(out=out_rows[:, t + 1 - rows : t + 1, starts[c] : starts[c] + w], in_=y[:, t + 1 - rows : t + 1, :])
 
         def planes(c):
             w = CHUNKS[c]
-            grouped = reuse.tile([P, w, PACK], BF16, name="y_grouped%d" % c, offset=16384 + 8 * starts[c], align_bytes=64)
-            nc.vector.tensor_copy(out=grouped[:].rearrange("p (c e) t -> p c t e", e=2),
+            if c < 2:
+                grouped = reuse.tile([P, w, PACK], BF16, name="y_grouped%d" % c, offset=20480 - 960 + 8 * starts[c], align_bytes=64)
+            else:
+                grouped = sbuf([P, w, PACK], BF16, "y_grouped%d" % c)
+            round_copy = nc.scalar.copy if c == len(CHUNKS) - 1 else nc.vector.tensor_copy
+            round_copy(out=grouped[:].rearrange("p (c e) t -> p c t e", e=2),
                                   in_=ys[c][:].rearrange("p t (c e) -> p c t e", e=2))
             first, last = [group for group in STORE_GROUPS if group[0] <= c <= group[1]][0]
             lo, hi = starts[first], starts[last] + CHUNKS[last]
@@ -196,13 +205,20 @@ def tile_list_tier_no_siluP_kernel(tc, xT, wgt, wt, b, offs, out_0, out_1, out_2
                 nc.sync.dma_start(out=out_words[:, lo:hi], in_=codes[:].bitcast(I32))
 
         n_chunks = len(CHUNKS)
-        front(0)
-        front(1)
-        for step in range(n_chunks):
-            quant_x(step)
-            if step + 2 < n_chunks:
-                front(step + 2)
-            multiply(step)
+        quant_x(0)
+        quant_x(1)
+        gather_all(3)
+        quant_x(2)
+        gather_all(4)
+        multiply(0, (0, 1, 2, 3))
+        multiply(1, (0, 1, 2, 3))
+        multiply(2, (0, 1))
+        weave_all(3)
+        multiply(2, (2, 3))
+        weave_all(4)
+        for c in (3, 4):
+            quant_x(c)
+            multiply(c, (0, 1, 2, 3))
         for step in range(n_chunks):
             planes(step)
         for quad in range(4):

@@ -20,7 +20,7 @@ SILU = mybir.ActivationFunctionType.Silu
 P = 128
 PACK = 4
 CHUNKS = (128, 256, 256, 256, 128)
-STORE_GROUPS = ((0, 1), (2, 2), (3, 3), (4, 4))
+STORE_GROUPS = ((0, 1), (2, 2), (3, 4))
 PARTS = ((0, 640), (640, 1024))
 
 

@@ -158,8 +158,9 @@ def tile_list_tier_no_siluP_kernel(tc, xT, wgt, wt, b, offs, out_0, out_1, out_2
                 gather(picked[c][:, i, :], i, starts[c], w)
 
         def weave_all(c):
-            nc.scalar.copy(out=xg[c][:].rearrange("p (c e) i -> p c i e", e=2),
-                           in_=picked[c][:].rearrange("p i (c e) -> p c i e", e=2))
+            copy = nc.vector.tensor_copy if c == 3 else nc.scalar.copy
+            copy(out=xg[c][:].rearrange("p (c e) i -> p c i e", e=2),
+                 in_=picked[c][:].rearrange("p i (c e) -> p c i e", e=2))
 
         def quant_x(c):
             w = CHUNKS[c]

@@ -121,25 +121,13 @@ def tile_list_tier_no_siluP_kernel(tc, xT, wgt, wt, b, offs, out_0, out_1, out_2
                                     in1=gate[h][:, j : j + width], op=MULT)
 
         early = PARTS[0][1]
-        low = reuse.tile([P, 2, early], F32, name="low", offset=3136)
-        for i in range(2):
-            gather(low[:, i, :], i, 0, early)
-        high = [reuse.tile([P, 2, CHUNKS[c]], F32, name="high%d" % c, offset=8256 + 8 * starts[c]) for c in range(3)]
+        picks = reuse.tile([P, PACK, early], F32, name="picks", offset=3136)
+        for i in range(PACK - 1):
+            gather(picks[:, i, :], i, 0, early)
         xg = [sbuf([P, CHUNKS[c], PACK], BF16, "xg%d" % c, tag="chunk%d" % c) for c in range(3)]
         xg.append(reuse.tile([P, CHUNKS[3], PACK], BF16, name="xg3", offset=20480, align_bytes=64))
         xg.append(sbuf([P, CHUNKS[4], PACK], BF16, "xg4"))
-
-        def weave_pair(c, pair, src):
-            nc.scalar.copy(out=xg[c][:, :, 2 * pair : 2 * pair + 2].rearrange("p (c e) i -> p c e i", e=4),
-                           in_=src.rearrange("p i (c e) -> p c e i", e=4))
-
-        for c in range(3):
-            weave_pair(c, 0, low[:, :, starts[c] : starts[c] + CHUNKS[c]])
-        for i in range(2, PACK):
-            for c in range(3):
-                gather(high[c][:, i - 2, :], i, starts[c], CHUNKS[c])
-        for c in range(3):
-            weave_pair(c, 1, high[c][:])
+        picked = {c: picks[:, :, starts[c] : starts[c] + CHUNKS[c]] for c in range(3)}
 
         out_rows = out_0.rearrange("(p t) j -> p t j", t=PACK)
         out_words = out_1.rearrange("a p j i -> p (a j i)").bitcast(I32)
@@ -149,18 +137,16 @@ def tile_list_tier_no_siluP_kernel(tc, xT, wgt, wt, b, offs, out_0, out_1, out_2
         ys = []
         y_codes = []
 
-        picked = {}
-
         def gather_all(c):
             w = CHUNKS[c]
-            picked[c] = sbuf([P, PACK, w], F32, "picked%d" % c, tag="chunk%d" % (c - 2))
+            picked[c] = sbuf([P, PACK, w], F32, "picked%d" % c, tag="chunk%d" % (c - 2))[:]
             for i in range(PACK):
                 gather(picked[c][:, i, :], i, starts[c], w)
 
         def weave_all(c):
             copy = nc.vector.tensor_copy if c == 3 else nc.scalar.copy
             copy(out=xg[c][:].rearrange("p (c e) i -> p c i e", e=2),
-                 in_=picked[c][:].rearrange("p i (c e) -> p c i e", e=2))
+                 in_=picked[c].rearrange("p i (c e) -> p c i e", e=2))
 
         def quant_x(c):
             w = CHUNKS[c]
@@ -206,12 +192,16 @@ def tile_list_tier_no_siluP_kernel(tc, xT, wgt, wt, b, offs, out_0, out_1, out_2
                 nc.sync.dma_start(out=out_words[:, lo:hi], in_=codes[:].bitcast(I32))
 
         n_chunks = len(CHUNKS)
-        quant_x(0)
-        quant_x(1)
+        for c in range(2):
+            gather(picked[c][:, 3, :], 3, starts[c], CHUNKS[c])
+            weave_all(c)
+            quant_x(c)
+        gather(picked[2][:, 3, :], 3, starts[2], CHUNKS[2])
         gather_all(3)
+        multiply(0, (0, 1, 2, 3))
+        weave_all(2)
         quant_x(2)
         gather_all(4)
-        multiply(0, (0, 1, 2, 3))
         multiply(1, (0, 1, 2, 3))
         multiply(2, (0, 1))
         weave_all(3)

@@ -20,7 +20,7 @@ SILU = mybir.ActivationFunctionType.Silu
 P = 128
 PACK = 4
 CHUNKS = (128, 256, 256, 256, 128)
-STORE_GROUPS = ((0, 1), (2, 2), (3, 4))
+STORE_GROUPS = ((0, 2), (3, 4))
 PARTS = ((0, 640), (640, 1024))
 
 
@@ -64,12 +64,14 @@ def tile_list_tier_no_siluP_kernel(tc, xT, wgt, wt, b, offs, out_0, out_1, out_2
         make_identity(nc, eye[:])
         eye_grouped = reuse.tile([P, PACK * (K + 1)], BF16, name="eye_grouped", offset=13440, align_bytes=64)
         nc.vector.memset(eye_grouped[:].bitcast(I32), 0)
-        nc.vector.tensor_copy(out=eye_grouped[:].rearrange("p (i r) -> p i r", i=PACK)[:, :, 0:K:PACK],
-                              in_=eye[:].unsqueeze(1).to_broadcast([P, PACK, P]))
+        eye_ones = eye_grouped[:].rearrange("p (i r) -> p i r", i=PACK)[:, :, 0:K:PACK]
         eye_codes = sbuf([P, K], U32, "eye_codes")
         eye_scales = sbuf([P, K], U8, "eye_scales")
-        nc.vector.quantize_mx(out=eye_codes[:].bitcast(FP8X4), scales=eye_scales[:],
-                              in_=eye_grouped[:, 0 : PACK * K])
+        for h in range(2):
+            nc.vector.tensor_copy(out=eye_ones[:, 2 * h : 2 * h + 2], in_=eye[:].unsqueeze(1).to_broadcast([P, 2, P]))
+        for h in range(2):
+            nc.vector.quantize_mx(out=eye_codes[:, 256 * h : 256 * (h + 1)].bitcast(FP8X4), scales=eye_scales[:, 256 * h : 256 * (h + 1)],
+                                  in_=eye_grouped[:, 1024 * h : 1024 * (h + 1)])
 
         rest_grouped = sbuf([P, PACK, P, PACK], BF16, "rest_grouped")
         main_grouped = sbuf([P, PACK, P, PACK], BF16, "main_grouped")

@@ -1,7 +1,6 @@
 from contextlib import ExitStack
 
 import concourse.mybir as mybir
-from concourse.masks import make_identity
 
 K, N, T, J = 512, 512, 2048, 1024
 FLOPS = 2 * 2 * K * N * J + 2 * K * K * N
@@ -14,14 +13,19 @@ U16 = mybir.dt.uint16
 U8 = mybir.dt.uint8
 FP8X4 = mybir.dt.float8_e4m3fn_x4
 MULT = mybir.AluOpType.mult
+ADD = mybir.AluOpType.add
+EQUAL = mybir.AluOpType.is_equal
 SUBTRACT = mybir.AluOpType.subtract
 SILU = mybir.ActivationFunctionType.Silu
 
 P = 128
 PACK = 4
-CHUNKS = (128, 256, 256, 256, 128)
-STORE_GROUPS = ((0, 2), (3, 4))
-PARTS = ((0, 640), (640, 1024))
+CHUNKS = (128, 256, 384, 256)
+EARLY = 768
+LATE = 3
+STORE_GROUPS = ((0, 384), (384, 768), (768, 1024))
+SCALAR_COLUMNS_X = (128, 256, 128, 0)
+SCALAR_COLUMNS_Y = (0, 0, 0, 64)
 
 
 def tile_list_tier_no_siluP_kernel(tc, xT, wgt, wt, b, offs, out_0, out_1, out_2):
@@ -32,27 +36,29 @@ def tile_list_tier_no_siluP_kernel(tc, xT, wgt, wt, b, offs, out_0, out_1, out_2
         reuse = ctx.enter_context(tc.tile_pool(name="reuse", bufs=1))
         psum = ctx.enter_context(tc.psum_pool(name="psum", bufs=8))
 
-        def sbuf(shape, dtype, name, tag=None):
-            return keep.tile(shape, dtype, name=name, tag=tag or name, align_bytes=64)
+        def sbuf(shape, dtype, name):
+            return keep.tile(shape, dtype, name=name, align_bytes=64)
+
+        def pairs(ap, layout):
+            return ap.rearrange("p %s -> p c i e" % layout, e=2)
 
         starts = [sum(CHUNKS[:c]) for c in range(len(CHUNKS))]
 
         offsets = lists.tile([P, J // 16], U16, name="offsets")
-        wt_rows = wt.rearrange("(p i) n -> p i n", i=PACK)
         x_rows = xT.rearrange("(p i) t -> p i t", i=PACK)
-        w_cols = ((0, 128), (128, 256), (256, 512))
-        w_raw = [reuse.tile([P, PACK, hi - lo], F32, name="w_raw%d" % lo, offset=4096 + 16 * lo) for lo, hi in w_cols]
+        picks = sbuf([P, PACK * EARLY + P], F32, "picks")
+        w_raw = (sbuf([P, PACK, 2 * P], F32, "w_raw")[:], picks[:, EARLY - P : EARLY - P + 2 * N].rearrange("p (i n) -> p i n", i=PACK))
         x_plane = [sbuf([P, T], F32, "x_plane%d" % i) for i in range(PACK)]
-        gate = [sbuf([P, hi - lo], F32, "gate%d" % lo) for lo, hi in PARTS]
+        gate = [sbuf([P, width], F32, "gate%d" % width) for width in (EARLY, J - EARLY)]
         bias = sbuf([P, PACK], F32, "bias")
-        for piece, (lo, hi) in zip(w_raw, w_cols):
-            nc.sync.dma_start(out=piece[:], in_=wt_rows[:, :, lo:hi])
+        for h in range(2):
+            nc.sync.dma_start(out=w_raw[h], in_=wt.rearrange("(p i) n -> p i n", i=PACK)[:, :, h * 2 * P : (h + 1) * 2 * P])
         nc.sync.dma_start(offsets[:], offs)
         nc.sync.dma_start(out=x_plane[0][:], in_=x_rows[:, 0, :])
-        nc.sync.dma_start(out=gate[0][:], in_=wgt[:, PARTS[0][0] : PARTS[0][1]])
+        nc.sync.dma_start(out=gate[0][:], in_=wgt[:, :EARLY])
         for i in range(1, PACK):
             nc.sync.dma_start(out=x_plane[i][:], in_=x_rows[:, i, :])
-        nc.sync.dma_start(out=gate[1][:], in_=wgt[:, PARTS[1][0] : PARTS[1][1]])
+        nc.sync.dma_start(out=gate[1][:], in_=wgt[:, EARLY:])
         nc.sync.dma_start(out=bias[:], in_=b.rearrange("(p t) -> p t", t=PACK))
 
         warm = sbuf([P, 1], F32, "warm")
@@ -60,160 +66,199 @@ def tile_list_tier_no_siluP_kernel(tc, xT, wgt, wt, b, offs, out_0, out_1, out_2
         warm_out = sbuf([P, 1], F32, "warm_out")
         nc.scalar.activation(out=warm_out[:], in_=warm[:], func=SILU)
 
-        eye = sbuf([P, P], BF16, "eye")
-        make_identity(nc, eye[:])
-        eye_grouped = reuse.tile([P, PACK * (K + 1)], BF16, name="eye_grouped", offset=13440, align_bytes=64)
-        nc.vector.memset(eye_grouped[:].bitcast(I32), 0)
-        eye_ones = eye_grouped[:].rearrange("p (i r) -> p i r", i=PACK)[:, :, 0:K:PACK]
-        eye_codes = sbuf([P, K], U32, "eye_codes")
-        eye_scales = sbuf([P, K], U8, "eye_scales")
-        for h in range(2):
-            nc.vector.tensor_copy(out=eye_ones[:, 2 * h : 2 * h + 2], in_=eye[:].unsqueeze(1).to_broadcast([P, 2, P]))
-        for h in range(2):
-            nc.vector.quantize_mx(out=eye_codes[:, 256 * h : 256 * (h + 1)].bitcast(FP8X4), scales=eye_scales[:, 256 * h : 256 * (h + 1)],
-                                  in_=eye_grouped[:, 1024 * h : 1024 * (h + 1)])
+        ones = sbuf([P, P], F32, "ones")
+        nc.vector.memset(ones[:], 1.0)
+        quadrant = sbuf([P, 1], F32, "quadrant")
+        for first in range(0, P, 32):
+            nc.vector.memset(quadrant[first : first + 32, :], -float(first))
+        column = sbuf([P, P], F32, "column")
+        nc.vector.tensor_tensor_scan(out=column[:], data0=ones[:], data1=ones[:], initial=0.0, op0=MULT, op1=ADD)
+        row = sbuf([P, 32], F32, "row")
+        nc.vector.transpose(out=row[:], in_=column[:, :32])
+        eye_in = reuse.tile([P, 2 * K + 4], BF16, name="eye_in", offset=0, align_bytes=64)
+        nc.vector.memset(eye_in[:].bitcast(I32), 0)
+        eye_high = sbuf([P, 2 * P + 1], U32, "eye_high")
+        eye_low = sbuf([P, 2 * P], U32, "eye_low")
+        eye_scales = sbuf([P, 2 * P], U8, "eye_scales")
+        plain_scales = sbuf([P, N], U8, "plain_scales")
+        nc.vector.memset(eye_high[:, 2 * P :], 0)
+        nc.vector.memset(plain_scales[:].bitcast(I32), 0)
+        eye_ones = eye_in[:, 2:].rearrange("p (r x) -> p r x", r=2)[:, :, 0:K:PACK]
+        nc.vector.tensor_scalar(out=eye_ones, in0=column[:].unsqueeze(1).to_broadcast([P, 2, P]), scalar1=quadrant[:], scalar2=row[:, 0:1],
+                                op0=ADD, op1=EQUAL)
+        nc.vector.quantize_mx(out=eye_high[:, : 2 * P].bitcast(FP8X4), scales=eye_scales[:], in_=eye_in[:, : 2 * K])
+        nc.scalar.copy(out=eye_low[:].bitcast(U16), in_=eye_high[:].bitcast(U16)[:, 1 : 4 * P + 1])
 
-        rest_grouped = sbuf([P, PACK, P, PACK], BF16, "rest_grouped")
-        main_grouped = sbuf([P, PACK, P, PACK], BF16, "main_grouped")
-        plains = []
-        rests = []
-        for q in range(4):
-            raw = w_raw[q][:] if q < 2 else w_raw[2][:, :, (q - 2) * P : (q - 1) * P]
-            plain = reuse.tile([P, P, PACK], BF16, name="plain%d" % q, offset=13440 + 1024 * q, align_bytes=64)
-            round_copy = nc.vector.tensor_copy if q == 0 else nc.scalar.copy
-            round_copy(out=plain[:].rearrange("p (c e) i -> p c i e", e=2),
-                           in_=raw.rearrange("p i (c e) -> p c i e", e=2))
-            plains.append(plain)
-            if q == 3:
-                codes = reuse.tile([P, P], U32, name="plain_codes3", offset=6144, align_bytes=64)
-            else:
-                codes = sbuf([P, P], U32, "plain_codes%d" % q)
-            scales = sbuf([P, P], U8, "plain_scales%d" % q)
-            nc.vector.quantize_mx(out=codes[:].bitcast(FP8X4), scales=scales[:],
-                                  in_=plain[:].rearrange("p n i -> p (n i)"))
-            values = psum.tile([P, PACK, P], F32, name="values", tag="bank")
-            for i in range(PACK):
-                nc.tensor.matmul_mx(out=values[:, i, :], lhsT=eye_codes[:, i * P : (i + 1) * P].bitcast(FP8X4),
-                                    lhsT_scale=eye_scales[:, i * P : (i + 1) * P],
-                                    rhs=codes[:].bitcast(FP8X4), rhs_scale=scales[:], start=True, stop=True)
-            rest = sbuf([P, P, PACK], BF16, "rest%d" % q)
-            rests.append(rest)
-            nc.vector.tensor_tensor(
-                out=rest[:].rearrange("p (c e) i -> p c i e", e=2),
-                in0=raw.rearrange("p i (c e) -> p c i e", e=2),
-                in1=values[:].rearrange("p i (c e) -> p c i e", e=2),
-                op=SUBTRACT)
-        for grouped, quarters in ((main_grouped, plains), (rest_grouped, rests)):
-            dealt = grouped[:].rearrange("p t m i -> p (t m i)").bitcast(F32).rearrange("p (t m e) -> p m t e", t=PACK, e=2)
-            for q in range(4):
-                nc.scalar.copy(out=dealt[:, 32 * q : 32 * (q + 1)],
-                               in_=quarters[q][:].rearrange("p n i -> p (n i)").bitcast(F32).rearrange("p (m t e) -> p m t e", t=PACK, e=2))
-        tiers = []
-        for name, grouped in (("main", main_grouped), ("rest", rest_grouped)):
-            codes = sbuf([P, N], U32, name + "_codes")
-            scales = sbuf([P, N], U8, name + "_scales")
-            nc.vector.quantize_mx(out=codes[:].bitcast(FP8X4), scales=scales[:],
-                                  in_=grouped[:].rearrange("p t m i -> p (t m i)"))
-            tiers.append((codes, scales))
+        plain = reuse.tile([P, 3 * K], BF16, name="plain", offset=0, align_bytes=64)
+        rounded = [plain[:, slot * K : (slot + 1) * K] for slot in (0, 1, 1, 2)]
+        plain_codes = sbuf([P, N], U32, "plain_codes")
+        raws = [w_raw[q // 2][:, :, (q % 2) * P : (q % 2 + 1) * P] for q in range(4)]
+        rest_dealt = (picks[:, 3 * EARLY + 160 : 3 * EARLY + 160 + N].bitcast(BF16),
+                      sbuf([P, 2 * N], BF16, "rest_dealt")[:])
+        rest_slots = [half.rearrange("p (e m i) -> p m i e", e=2, i=PACK) for half in rest_dealt]
+        values = {}
 
-        def gather(dst, i, j0, width):
-            h = 0 if j0 < PARTS[1][0] else 1
-            j = j0 - PARTS[h][0]
-            nc.vector.tensor_tensor(out=dst, in0=x_plane[i][:].indirect(offsets[:, j0 // 16 : (j0 + width) // 16]),
-                                    in1=gate[h][:, j : j + width], op=MULT)
+        def round_w(q):
+            copy = nc.vector.tensor_copy if q % 2 == 0 else nc.scalar.copy
+            copy(out=rounded[q].rearrange("p (u e m i) -> p u m i e", u=2, e=2, i=PACK),
+                 in_=raws[q].rearrange("p i (m u e) -> p u m i e", u=2, e=2))
 
-        early = PARTS[0][1]
-        picks = reuse.tile([P, PACK, early], F32, name="picks", offset=3136)
+        def quantise_w(q):
+            cols = slice(q * P, (q + 1) * P)
+            nc.vector.quantize_mx(out=plain_codes[:, cols].bitcast(FP8X4), scales=plain_scales[:, cols], in_=rounded[q])
+            values[q] = psum.tile([P, PACK, P], F32, name="values", tag="bank")
+            for i in (2, 3, 0, 1):
+                eye_codes = eye_high if i >= 2 else eye_low
+                part = slice((i % 2) * P, (i % 2 + 1) * P)
+                nc.tensor.matmul_mx(out=values[q][:, i, :], lhsT=eye_codes[:, part].bitcast(FP8X4), lhsT_scale=eye_scales[:, part],
+                                    rhs=plain_codes[:, cols].bitcast(FP8X4), rhs_scale=plain_scales[:, cols], start=True, stop=True)
+
+        def subtract_w(q):
+            for u in range(2):
+                nc.vector.tensor_tensor(out=rest_slots[u][:, 32 * q : 32 * (q + 1)],
+                                        in0=raws[q].rearrange("p i (m u e) -> p u m i e", u=2, e=2)[:, u],
+                                        in1=values[q][:].rearrange("p i (u e m) -> p u m i e", u=2, e=2)[:, u], op=SUBTRACT)
+
+        round_w(0)
+        round_w(1)
+        round_w(3)
+        quantise_w(0)
+        quantise_w(1)
+        round_w(2)
+        subtract_w(0)
+        quantise_w(2)
+        quantise_w(3)
+        subtract_w(1)
+        subtract_w(2)
+        main_codes = sbuf([P, N], U32, "main_codes")
+        main_scales = sbuf([P, N], U8, "main_scales")
+
+        def deal(dealt, by_quarter):
+            nc.scalar.copy(out=dealt.rearrange("p (t q m) -> p q t m", t=PACK, q=4), in_=by_quarter.rearrange("p (q t m) -> p q t m", t=PACK, q=4))
+
+        deal(main_codes[:], plain_codes[:])
+        deal(main_scales[:].bitcast(U32), plain_scales[:].bitcast(U32))
+        subtract_w(3)
+
+        rest_codes = sbuf([P, N], U32, "rest_codes")
+        rest_scales = sbuf([P, N], U8, "rest_scales")
+        tiers = ((main_codes, main_scales), (rest_codes, rest_scales))
+
+        picked = picks[:, : PACK * EARLY].rearrange("p (i j) -> p i j", i=PACK)
+        late = picks[:, P:].rearrange("p (a b j) -> p b a j", a=2, b=3)[:, :2, :, : J - EARLY]
+
+        def gather(i, j0, width):
+            dst, weights = (picked[:, i, j0 : j0 + width], gate[0][:, j0 : j0 + width]) if j0 < EARLY else (late[:, i // 2, i % 2], gate[1][:])
+            nc.vector.tensor_tensor(out=dst, in0=x_plane[i][:].indirect(offsets[:, j0 // 16 : (j0 + width) // 16]), in1=weights, op=MULT)
+
+        def quantise_rest(u):
+            cols = slice(u * 2 * P, (u + 1) * 2 * P)
+            nc.vector.quantize_mx(out=rest_codes[:, cols].bitcast(FP8X4), scales=rest_scales[:, cols], in_=rest_dealt[u])
+
+        quantise_rest(0)
+        quantise_rest(1)
         for i in range(PACK - 1):
-            gather(picks[:, i, :], i, 0, early)
-        xg = [sbuf([P, CHUNKS[c], PACK], BF16, "xg%d" % c, tag="chunk%d" % c) for c in range(3)]
-        xg.append(reuse.tile([P, CHUNKS[3], PACK], BF16, name="xg3", offset=20480, align_bytes=64))
-        xg.append(sbuf([P, CHUNKS[4], PACK], BF16, "xg4"))
-        picked = {c: picks[:, :, starts[c] : starts[c] + CHUNKS[c]] for c in range(3)}
+            gather(i, 0, EARLY)
 
         out_rows = out_0.rearrange("(p t) j -> p t j", t=PACK)
         out_words = out_1.rearrange("a p j i -> p (a j i)").bitcast(I32)
         out_scales = out_2.rearrange("a q j -> (a q) j").bitcast(I32)
         y_scales = sbuf([P, J], U8, "y_scales")
-        xq = []
-        ys = []
-        y_codes = []
+        xg = {}
+        xq = {}
+        ys = {}
 
-        def gather_all(c):
-            w = CHUNKS[c]
-            picked[c] = sbuf([P, PACK, w], F32, "picked%d" % c, tag="chunk%d" % (c - 2))[:]
-            for i in range(PACK):
-                gather(picked[c][:, i, :], i, starts[c], w)
+        def weave(engine, dst, src, scalar_columns):
+            split = src.shape[2] - scalar_columns
+            lo, hi = (0, split) if engine is nc.vector else (split, src.shape[2])
+            copy = nc.vector.tensor_copy if engine is nc.vector else nc.scalar.copy
+            copy(out=pairs(dst[:, lo:hi], "(c e) i"), in_=pairs(src[:, :, lo:hi], "i (c e)"))
 
-        def weave_all(c):
-            copy = nc.vector.tensor_copy if c == 3 else nc.scalar.copy
-            copy(out=xg[c][:].rearrange("p (c e) i -> p c i e", e=2),
-                 in_=picked[c].rearrange("p i (c e) -> p c i e", e=2))
+        for c, w in enumerate(CHUNKS):
+            xg[c] = sbuf([P, w * PACK], BF16, "xg%d" % c)[:]
 
-        def quant_x(c):
+        def weave_x(c, engine):
+            if c == LATE:
+                nc.vector.tensor_copy(out=xg[c].rearrange("p (c e b a) -> p c b a e", e=2, b=2, a=2), in_=late.rearrange("p b a (c e) -> p c b a e", e=2))
+            else:
+                weave(engine, xg[c].rearrange("p (j i) -> p j i", i=PACK), picked[:, :, starts[c] : starts[c] + CHUNKS[c]], SCALAR_COLUMNS_X[c])
+
+        def quantise_x(c):
             w = CHUNKS[c]
             codes = sbuf([P, w], U32, "xg_codes%d" % c)
             scales = sbuf([P, w], U8, "xg_scales%d" % c)
-            nc.vector.quantize_mx(out=codes[:].bitcast(FP8X4), scales=scales[:], in_=xg[c][:].rearrange("p j i -> p (j i)"))
-            xq.append((codes, scales))
+            nc.vector.quantize_mx(out=codes[:].bitcast(FP8X4), scales=scales[:], in_=xg[c])
+            xq[c] = (codes, scales)
 
-        def multiply(c, slots):
+        def multiply(c):
             w = CHUNKS[c]
             codes, scales = xq[c]
-            if slots[0] == 0:
-                ys.append(sbuf([P, PACK, w], F32, "y%d" % c))
-            y = ys[c]
-            for t in slots:
+            y = sbuf([P, PACK, w], F32, "y%d" % c)
+            ys[c] = y
+            for t in range(PACK):
                 acc = psum.tile([P, w], F32, name="acc", tag="bank")
-                for n, (w_codes, w_scales) in enumerate(tiers):
-                    nc.tensor.matmul_mx(out=acc[:], lhsT=w_codes[:, t * P : (t + 1) * P].bitcast(FP8X4),
-                                        lhsT_scale=w_scales[:, t * P : (t + 1) * P],
-                                        rhs=codes[:].bitcast(FP8X4), rhs_scale=scales[:], start=(n == 0), stop=(n == 1))
+                for lo in range(0, w, 256):
+                    cols = slice(lo, min(lo + 256, w))
+                    for n, (w_codes, w_scales) in enumerate(tiers):
+                        nc.tensor.matmul_mx(out=acc[:, cols], lhsT=w_codes[:, t * P : (t + 1) * P].bitcast(FP8X4),
+                                            lhsT_scale=w_scales[:, t * P : (t + 1) * P],
+                                            rhs=codes[:, cols].bitcast(FP8X4), rhs_scale=scales[:, cols], start=(n == 0), stop=(n == 1))
                 nc.scalar.activation(out=y[:, t, :], in_=acc[:], func=SILU, bias=bias[:, t : t + 1])
                 rows = 512 // w
                 if (t + 1) % rows == 0:
                     nc.sync.dma_start(out=out_rows[:, t + 1 - rows : t + 1, starts[c] : starts[c] + w], in_=y[:, t + 1 - rows : t + 1, :])
 
-        def planes(c):
-            w = CHUNKS[c]
-            if c < 2:
-                grouped = reuse.tile([P, w, PACK], BF16, name="y_grouped%d" % c, offset=20480 - 960 + 8 * starts[c], align_bytes=64)
-            else:
-                grouped = sbuf([P, w, PACK], BF16, "y_grouped%d" % c)
-            round_copy = nc.scalar.copy if c == len(CHUNKS) - 1 else nc.vector.tensor_copy
-            round_copy(out=grouped[:].rearrange("p (c e) t -> p c t e", e=2),
-                                  in_=ys[c][:].rearrange("p t (c e) -> p c t e", e=2))
-            first, last = [group for group in STORE_GROUPS if group[0] <= c <= group[1]][0]
-            lo, hi = starts[first], starts[last] + CHUNKS[last]
-            if c == first:
-                y_codes.append(sbuf([P, hi - lo], U32, "y_codes%d" % c))
-            codes = y_codes[-1]
-            nc.vector.quantize_mx(out=codes[:, starts[c] - lo : starts[c] - lo + w].bitcast(FP8X4), scales=y_scales[:, starts[c] : starts[c] + w],
-                                  in_=grouped[:].rearrange("p j t -> p (j t)"))
-            if c == last:
-                nc.sync.dma_start(out=out_words[:, lo:hi], in_=codes[:].bitcast(I32))
+        y_codes = [sbuf([P, hi - lo], U32, "y_codes%d" % lo) for lo, hi in STORE_GROUPS]
+        grouped = [picks[:, first : first + 2 * CHUNKS[c]].bitcast(BF16).rearrange("p (j i) -> p j i", i=PACK) for c, first in enumerate((1408, 128))]
+        grouped.extend(sbuf([P, CHUNKS[c], PACK], BF16, "y_grouped%d" % c)[:] for c in (2, 3))
 
-        n_chunks = len(CHUNKS)
-        for c in range(2):
-            gather(picked[c][:, 3, :], 3, starts[c], CHUNKS[c])
-            weave_all(c)
-            quant_x(c)
-        gather(picked[2][:, 3, :], 3, starts[2], CHUNKS[2])
-        gather_all(3)
-        multiply(0, (0, 1, 2, 3))
-        weave_all(2)
-        quant_x(2)
-        gather_all(4)
-        multiply(1, (0, 1, 2, 3))
-        multiply(2, (0, 1))
-        weave_all(3)
-        multiply(2, (2, 3))
-        weave_all(4)
-        for c in (3, 4):
-            quant_x(c)
-            multiply(c, (0, 1, 2, 3))
-        for step in range(n_chunks):
-            planes(step)
+        def weave_y(c, engine):
+            weave(engine, grouped[c], ys[c][:], SCALAR_COLUMNS_Y[c])
+
+        def quantise_y(c):
+            w = CHUNKS[c]
+            g = max(c - 1, 0)
+            lo = starts[c] - STORE_GROUPS[g][0]
+            nc.vector.quantize_mx(out=y_codes[g][:, lo : lo + w].bitcast(FP8X4), scales=y_scales[:, starts[c] : starts[c] + w],
+                                  in_=grouped[c].rearrange("p j t -> p (j t)"))
+
+        def store_words(g):
+            lo, hi = STORE_GROUPS[g]
+            nc.sync.dma_start(out=out_words[:, lo:hi], in_=y_codes[g][:].bitcast(I32))
+
+        gather(3, 0, 128)
+        weave_x(0, nc.scalar)
+        gather(3, 128, 256)
+        weave_x(1, nc.scalar)
+        gather(3, 384, 256)
+        quantise_x(0)
+        multiply(0)
+        gather(3, 640, 128)
+        weave_x(2, nc.vector)
+        quantise_x(1)
+        weave_x(2, nc.scalar)
+        multiply(1)
+        gather(0, EARLY, 256)
+        gather(1, EARLY, 256)
+        quantise_x(2)
+        multiply(2)
+        gather(2, EARLY, 256)
+        gather(3, EARLY, 256)
+        weave_y(0, nc.vector)
+        weave_x(3, nc.vector)
+        quantise_y(0)
+        quantise_x(3)
+        multiply(3)
+        weave_y(1, nc.vector)
+        weave_y(2, nc.vector)
+        quantise_y(1)
+        store_words(0)
+        quantise_y(2)
+        store_words(1)
+        weave_y(3, nc.scalar)
+        weave_y(3, nc.vector)
+        quantise_y(3)
+        store_words(2)
         for quad in range(4):
             queue = nc.sync if quad % 2 == 0 else nc.scalar
             queue.dma_start(out=out_scales[4 * quad : 4 * quad + 4, :],

@@ -24,8 +24,8 @@ CHUNKS = (128, 256, 384, 256)
 EARLY = 768
 LATE = 3
 STORE_GROUPS = ((0, 384), (384, 768), (768, 1024))
-SCALAR_COLUMNS_X = (128, 256, 128, 0)
-SCALAR_COLUMNS_Y = (0, 0, 0, 64)
+SHARES_X = {1: ((0, 128), (128, 256)), 2: ((0, 256), (256, 384))}
+SHARES_Y = {3: ((192, 256), (0, 192))}
 
 
 def tile_list_tier_no_siluP_kernel(tc, xT, wgt, wt, b, offs, out_0, out_1, out_2):
@@ -46,7 +46,7 @@ def tile_list_tier_no_siluP_kernel(tc, xT, wgt, wt, b, offs, out_0, out_1, out_2
 
         offsets = lists.tile([P, J // 16], U16, name="offsets")
         x_rows = xT.rearrange("(p i) t -> p i t", i=PACK)
-        picks = sbuf([P, PACK * EARLY + P], F32, "picks")
+        picks = sbuf([P, PACK * EARLY], F32, "picks")
         w_raw = (sbuf([P, PACK, 2 * P], F32, "w_raw")[:], picks[:, EARLY - P : EARLY - P + 2 * N].rearrange("p (i n) -> p i n", i=PACK))
         x_plane = [sbuf([P, T], F32, "x_plane%d" % i) for i in range(PACK)]
         gate = [sbuf([P, width], F32, "gate%d" % width) for width in (EARLY, J - EARLY)]
@@ -144,11 +144,11 @@ def tile_list_tier_no_siluP_kernel(tc, xT, wgt, wt, b, offs, out_0, out_1, out_2
         rest_scales = sbuf([P, N], U8, "rest_scales")
         tiers = ((main_codes, main_scales), (rest_codes, rest_scales))
 
-        picked = picks[:, : PACK * EARLY].rearrange("p (i j) -> p i j", i=PACK)
-        late = picks[:, P:].rearrange("p (a b j) -> p b a j", a=2, b=3)[:, :2, :, : J - EARLY]
+        picked = picks[:].rearrange("p (i j) -> p i j", i=PACK)
+        late = picked[:, :, starts[2] : starts[2] + CHUNKS[LATE]]
 
         def gather(i, j0, width):
-            dst, weights = (picked[:, i, j0 : j0 + width], gate[0][:, j0 : j0 + width]) if j0 < EARLY else (late[:, i // 2, i % 2], gate[1][:])
+            dst, weights = (picked[:, i, j0 : j0 + width], gate[0][:, j0 : j0 + width]) if j0 < EARLY else (late[:, i], gate[1][:])
             nc.vector.tensor_tensor(out=dst, in0=x_plane[i][:].indirect(offsets[:, j0 // 16 : (j0 + width) // 16]), in1=weights, op=MULT)
 
         def quantise_rest(u):
@@ -168,9 +168,8 @@ def tile_list_tier_no_siluP_kernel(tc, xT, wgt, wt, b, offs, out_0, out_1, out_2
         xq = {}
         ys = {}
 
-        def weave(engine, dst, src, scalar_columns):
-            split = src.shape[2] - scalar_columns
-            lo, hi = (0, split) if engine is nc.vector else (split, src.shape[2])
+        def weave(engine, dst, src, shares):
+            lo, hi = (0, src.shape[2]) if shares is None else shares[1 if engine is nc.vector else 0]
             copy = nc.vector.tensor_copy if engine is nc.vector else nc.scalar.copy
             copy(out=pairs(dst[:, lo:hi], "(c e) i"), in_=pairs(src[:, :, lo:hi], "i (c e)"))
 
@@ -178,10 +177,8 @@ def tile_list_tier_no_siluP_kernel(tc, xT, wgt, wt, b, offs, out_0, out_1, out_2
             xg[c] = sbuf([P, w * PACK], BF16, "xg%d" % c)[:]
 
         def weave_x(c, engine):
-            if c == LATE:
-                nc.vector.tensor_copy(out=xg[c].rearrange("p (c e b a) -> p c b a e", e=2, b=2, a=2), in_=late.rearrange("p b a (c e) -> p c b a e", e=2))
-            else:
-                weave(engine, xg[c].rearrange("p (j i) -> p j i", i=PACK), picked[:, :, starts[c] : starts[c] + CHUNKS[c]], SCALAR_COLUMNS_X[c])
+            src = late if c == LATE else picked[:, :, starts[c] : starts[c] + CHUNKS[c]]
+            weave(engine, xg[c].rearrange("p (j i) -> p j i", i=PACK), src, SHARES_X.get(c))
 
         def quantise_x(c):
             w = CHUNKS[c]
@@ -209,11 +206,11 @@ def tile_list_tier_no_siluP_kernel(tc, xT, wgt, wt, b, offs, out_0, out_1, out_2
                     nc.sync.dma_start(out=out_rows[:, t + 1 - rows : t + 1, starts[c] : starts[c] + w], in_=y[:, t + 1 - rows : t + 1, :])
 
         y_codes = [sbuf([P, hi - lo], U32, "y_codes%d" % lo) for lo, hi in STORE_GROUPS]
-        grouped = [picks[:, first : first + 2 * CHUNKS[c]].bitcast(BF16).rearrange("p (j i) -> p j i", i=PACK) for c, first in enumerate((1408, 128))]
-        grouped.extend(sbuf([P, CHUNKS[c], PACK], BF16, "y_grouped%d" % c)[:] for c in (2, 3))
+        grouped = {c: sbuf([P, CHUNKS[c], PACK], BF16, "y_grouped%d" % c)[:] for c in (0, 2, 3)}
+        grouped[1] = picks[:, starts[2] : starts[2] + 2 * CHUNKS[1]].bitcast(BF16).rearrange("p (j i) -> p j i", i=PACK)
 
         def weave_y(c, engine):
-            weave(engine, grouped[c], ys[c][:], SCALAR_COLUMNS_Y[c])
+            weave(engine, grouped[c], ys[c][:], SHARES_Y.get(c))
 
         def quantise_y(c):
             w = CHUNKS[c]
@@ -231,19 +228,18 @@ def tile_list_tier_no_siluP_kernel(tc, xT, wgt, wt, b, offs, out_0, out_1, out_2
         gather(3, 128, 256)
         weave_x(1, nc.scalar)
         gather(3, 384, 256)
+        weave_x(2, nc.scalar)
         quantise_x(0)
         multiply(0)
+        weave_x(1, nc.vector)
         gather(3, 640, 128)
-        weave_x(2, nc.vector)
         quantise_x(1)
-        weave_x(2, nc.scalar)
         multiply(1)
-        gather(0, EARLY, 256)
-        gather(1, EARLY, 256)
+        weave_x(2, nc.vector)
         quantise_x(2)
         multiply(2)
-        gather(2, EARLY, 256)
-        gather(3, EARLY, 256)
+        for i in range(PACK):
+            gather(i, EARLY, 256)
         weave_y(0, nc.vector)
         weave_x(3, nc.vector)
         quantise_y(0)

@@ -25,7 +25,6 @@ EARLY = 768
 LATE = 3
 STORE_GROUPS = ((0, 384), (384, 768), (768, 1024))
 SHARES_X = {1: ((0, 128), (128, 256)), 2: ((0, 256), (256, 384))}
-SHARES_Y = {3: ((192, 256), (0, 192))}
 
 
 def tile_list_tier_no_siluP_kernel(tc, xT, wgt, wt, b, offs, out_0, out_1, out_2):
@@ -92,7 +91,7 @@ def tile_list_tier_no_siluP_kernel(tc, xT, wgt, wt, b, offs, out_0, out_1, out_2
         plain = reuse.tile([P, 3 * K], BF16, name="plain", offset=0, align_bytes=64)
         rounded = [plain[:, slot * K : (slot + 1) * K] for slot in (0, 1, 1, 2)]
         plain_codes = sbuf([P, N], U32, "plain_codes")
-        raws = [w_raw[q // 2][:, :, (q % 2) * P : (q % 2 + 1) * P] for q in range(4)]
+        raws = [w_raw[q // 2].rearrange("p i (m u e) -> p u m i e", u=2, e=2)[:, q % 2] for q in range(4)]
         rest_dealt = (picks[:, 3 * EARLY + 160 : 3 * EARLY + 160 + N].bitcast(BF16),
                       sbuf([P, 2 * N], BF16, "rest_dealt")[:])
         rest_slots = [half.rearrange("p (e m i) -> p m i e", e=2, i=PACK) for half in rest_dealt]
@@ -100,8 +99,7 @@ def tile_list_tier_no_siluP_kernel(tc, xT, wgt, wt, b, offs, out_0, out_1, out_2
 
         def round_w(q):
             copy = nc.vector.tensor_copy if q % 2 == 0 else nc.scalar.copy
-            copy(out=rounded[q].rearrange("p (u e m i) -> p u m i e", u=2, e=2, i=PACK),
-                 in_=raws[q].rearrange("p i (m u e) -> p u m i e", u=2, e=2))
+            copy(out=rounded[q].rearrange("p (e m i) -> p m i e", e=2, i=PACK), in_=raws[q])
 
         def quantise_w(q):
             cols = slice(q * P, (q + 1) * P)
@@ -114,10 +112,10 @@ def tile_list_tier_no_siluP_kernel(tc, xT, wgt, wt, b, offs, out_0, out_1, out_2
                                     rhs=plain_codes[:, cols].bitcast(FP8X4), rhs_scale=plain_scales[:, cols], start=True, stop=True)
 
         def subtract_w(q):
-            for u in range(2):
-                nc.vector.tensor_tensor(out=rest_slots[u][:, 32 * q : 32 * (q + 1)],
-                                        in0=raws[q].rearrange("p i (m u e) -> p u m i e", u=2, e=2)[:, u],
-                                        in1=values[q][:].rearrange("p i (u e m) -> p u m i e", u=2, e=2)[:, u], op=SUBTRACT)
+            step = 32 if q == 0 else 64
+            for lo in range(0, 64, step):
+                nc.vector.tensor_tensor(out=rest_slots[q % 2][:, 64 * (q // 2) + lo : 64 * (q // 2) + lo + step], in0=raws[q][:, lo : lo + step],
+                                        in1=values[q][:].rearrange("p i (e m) -> p m i e", e=2)[:, lo : lo + step], op=SUBTRACT)
 
         round_w(0)
         round_w(1)
@@ -134,7 +132,7 @@ def tile_list_tier_no_siluP_kernel(tc, xT, wgt, wt, b, offs, out_0, out_1, out_2
         main_scales = sbuf([P, N], U8, "main_scales")
 
         def deal(dealt, by_quarter):
-            nc.scalar.copy(out=dealt.rearrange("p (t q m) -> p q t m", t=PACK, q=4), in_=by_quarter.rearrange("p (q t m) -> p q t m", t=PACK, q=4))
+            nc.scalar.copy(out=dealt.rearrange("p (t h m) -> p h t m", t=PACK, h=2), in_=by_quarter.rearrange("p (h t m) -> p h t m", t=PACK, h=2))
 
         deal(main_codes[:], plain_codes[:])
         deal(main_scales[:].bitcast(U32), plain_scales[:].bitcast(U32))
@@ -201,7 +199,7 @@ def tile_list_tier_no_siluP_kernel(tc, xT, wgt, wt, b, offs, out_0, out_1, out_2
                                             lhsT_scale=w_scales[:, t * P : (t + 1) * P],
                                             rhs=codes[:, cols].bitcast(FP8X4), rhs_scale=scales[:, cols], start=(n == 0), stop=(n == 1))
                 nc.scalar.activation(out=y[:, t, :], in_=acc[:], func=SILU, bias=bias[:, t : t + 1])
-                rows = 512 // w
+                rows = 4 if w == 128 else 2
                 if (t + 1) % rows == 0:
                     nc.sync.dma_start(out=out_rows[:, t + 1 - rows : t + 1, starts[c] : starts[c] + w], in_=y[:, t + 1 - rows : t + 1, :])
 
@@ -209,15 +207,16 @@ def tile_list_tier_no_siluP_kernel(tc, xT, wgt, wt, b, offs, out_0, out_1, out_2
         grouped = {c: sbuf([P, CHUNKS[c], PACK], BF16, "y_grouped%d" % c)[:] for c in (0, 2, 3)}
         grouped[1] = picks[:, starts[2] : starts[2] + 2 * CHUNKS[1]].bitcast(BF16).rearrange("p (j i) -> p j i", i=PACK)
 
-        def weave_y(c, engine):
-            weave(engine, grouped[c], ys[c][:], SHARES_Y.get(c))
+        def weave_y(c, engine, lo=0, hi=None):
+            share = (lo, hi or CHUNKS[c])
+            weave(engine, grouped[c], ys[c][:], (share, share))
 
-        def quantise_y(c):
-            w = CHUNKS[c]
+        def quantise_y(c, lo=0, hi=None):
+            hi = hi or CHUNKS[c]
             g = max(c - 1, 0)
-            lo = starts[c] - STORE_GROUPS[g][0]
-            nc.vector.quantize_mx(out=y_codes[g][:, lo : lo + w].bitcast(FP8X4), scales=y_scales[:, starts[c] : starts[c] + w],
-                                  in_=grouped[c].rearrange("p j t -> p (j t)"))
+            first = starts[c] - STORE_GROUPS[g][0]
+            nc.vector.quantize_mx(out=y_codes[g][:, first + lo : first + hi].bitcast(FP8X4), scales=y_scales[:, starts[c] + lo : starts[c] + hi],
+                                  in_=grouped[c][:, lo:hi].rearrange("p j t -> p (j t)"))
 
         def store_words(g):
             lo, hi = STORE_GROUPS[g]
@@ -246,13 +245,15 @@ def tile_list_tier_no_siluP_kernel(tc, xT, wgt, wt, b, offs, out_0, out_1, out_2
         quantise_x(3)
         multiply(3)
         weave_y(1, nc.vector)
-        weave_y(2, nc.vector)
         quantise_y(1)
         store_words(0)
-        quantise_y(2)
+        weave_y(2, nc.vector, 0, 256)
+        weave_y(2, nc.vector, 256, 384)
+        quantise_y(2, 0, 256)
+        weave_y(3, nc.scalar, 160, 256)
+        weave_y(3, nc.vector, 0, 160)
+        quantise_y(2, 256, 384)
         store_words(1)
-        weave_y(3, nc.scalar)
-        weave_y(3, nc.vector)
         quantise_y(3)
         store_words(2)
         for quad in range(4):

@@ -24,7 +24,6 @@ CHUNKS = (128, 256, 384, 256)
 EARLY = 768
 LATE = 3
 STORE_GROUPS = ((0, 384), (384, 768), (768, 1024))
-SHARES_X = {1: ((0, 128), (128, 256)), 2: ((0, 256), (256, 384))}
 
 
 def tile_list_tier_no_siluP_kernel(tc, xT, wgt, wt, b, offs, out_0, out_1, out_2):
@@ -143,10 +142,10 @@ def tile_list_tier_no_siluP_kernel(tc, xT, wgt, wt, b, offs, out_0, out_1, out_2
         tiers = ((main_codes, main_scales), (rest_codes, rest_scales))
 
         picked = picks[:].rearrange("p (i j) -> p i j", i=PACK)
-        late = picked[:, :, starts[2] : starts[2] + CHUNKS[LATE]]
+        late = picked[:, 2:, starts[1] : starts[1] + 2 * CHUNKS[LATE]].rearrange("p a (b j) -> p b a j", b=2)
 
         def gather(i, j0, width):
-            dst, weights = (picked[:, i, j0 : j0 + width], gate[0][:, j0 : j0 + width]) if j0 < EARLY else (late[:, i], gate[1][:])
+            dst, weights = (picked[:, i, j0 : j0 + width], gate[0][:, j0 : j0 + width]) if j0 < EARLY else (late[:, i // 2, i % 2], gate[1][:])
             nc.vector.tensor_tensor(out=dst, in0=x_plane[i][:].indirect(offsets[:, j0 // 16 : (j0 + width) // 16]), in1=weights, op=MULT)
 
         def quantise_rest(u):
@@ -155,8 +154,10 @@ def tile_list_tier_no_siluP_kernel(tc, xT, wgt, wt, b, offs, out_0, out_1, out_2
 
         quantise_rest(0)
         quantise_rest(1)
-        for i in range(PACK - 1):
-            gather(i, 0, EARLY)
+        gather(0, 0, EARLY)
+        gather(1, 0, EARLY // 2)
+        gather(1, EARLY // 2, EARLY // 2)
+        gather(2, 0, EARLY)
 
         out_rows = out_0.rearrange("(p t) j -> p t j", t=PACK)
         out_words = out_1.rearrange("a p j i -> p (a j i)").bitcast(I32)
@@ -174,9 +175,16 @@ def tile_list_tier_no_siluP_kernel(tc, xT, wgt, wt, b, offs, out_0, out_1, out_2
         for c, w in enumerate(CHUNKS):
             xg[c] = sbuf([P, w * PACK], BF16, "xg%d" % c)[:]
 
-        def weave_x(c, engine):
-            src = late if c == LATE else picked[:, :, starts[c] : starts[c] + CHUNKS[c]]
-            weave(engine, xg[c].rearrange("p (j i) -> p j i", i=PACK), src, SHARES_X.get(c))
+        def weave_x(c, engine, lo, hi, planes):
+            dst = xg[c].rearrange("p (j i) -> p j i", i=PACK)[:, :, planes]
+            weave(engine, dst, picked[:, planes, starts[c] : starts[c] + CHUNKS[c]], ((lo, hi), (lo, hi)))
+
+        def weave_late():
+            nc.vector.tensor_copy(out=xg[LATE].rearrange("p (c e b a) -> p c b a e", e=2, b=2, a=2), in_=late.rearrange("p b a (c e) -> p c b a e", e=2))
+
+        low, high = slice(0, 2), slice(2, 4)
+        for c in range(LATE):
+            weave_x(c, nc.scalar, 0, CHUNKS[c], low)
 
         def quantise_x(c):
             w = CHUNKS[c]
@@ -205,7 +213,7 @@ def tile_list_tier_no_siluP_kernel(tc, xT, wgt, wt, b, offs, out_0, out_1, out_2
 
         y_codes = [sbuf([P, hi - lo], U32, "y_codes%d" % lo) for lo, hi in STORE_GROUPS]
         grouped = {c: sbuf([P, CHUNKS[c], PACK], BF16, "y_grouped%d" % c)[:] for c in (0, 2, 3)}
-        grouped[1] = picks[:, starts[2] : starts[2] + 2 * CHUNKS[1]].bitcast(BF16).rearrange("p (j i) -> p j i", i=PACK)
+        grouped[1] = picks[:, 2 * EARLY + starts[1] : 2 * EARLY + starts[1] + 2 * CHUNKS[1]].bitcast(BF16).rearrange("p (j i) -> p j i", i=PACK)
 
         def weave_y(c, engine, lo=0, hi=None):
             share = (lo, hi or CHUNKS[c])
@@ -223,24 +231,23 @@ def tile_list_tier_no_siluP_kernel(tc, xT, wgt, wt, b, offs, out_0, out_1, out_2
             nc.sync.dma_start(out=out_words[:, lo:hi], in_=y_codes[g][:].bitcast(I32))
 
         gather(3, 0, 128)
-        weave_x(0, nc.scalar)
+        weave_x(0, nc.scalar, 0, 128, high)
         gather(3, 128, 256)
-        weave_x(1, nc.scalar)
+        weave_x(1, nc.scalar, 0, 256, high)
         gather(3, 384, 256)
-        weave_x(2, nc.scalar)
+        weave_x(2, nc.scalar, 0, 256, high)
         quantise_x(0)
         multiply(0)
-        weave_x(1, nc.vector)
         gather(3, 640, 128)
         quantise_x(1)
         multiply(1)
-        weave_x(2, nc.vector)
+        weave_x(2, nc.vector, 256, 384, high)
         quantise_x(2)
         multiply(2)
         for i in range(PACK):
             gather(i, EARLY, 256)
         weave_y(0, nc.vector)
-        weave_x(3, nc.vector)
+        weave_late()
         quantise_y(0)
         quantise_x(3)
         multiply(3)

@@ -40,6 +40,7 @@ def tile_list_tier_no_siluP_kernel(tc, xT, wgt, wt, b, offs, out_0, out_1, out_2
         def pairs(ap, layout):
             return ap.rearrange("p %s -> p c i e" % layout, e=2)
 
+
         starts = [sum(CHUNKS[:c]) for c in range(len(CHUNKS))]
 
         offsets = lists.tile([P, J // 16], U16, name="offsets")
@@ -59,31 +60,28 @@ def tile_list_tier_no_siluP_kernel(tc, xT, wgt, wt, b, offs, out_0, out_1, out_2
         nc.sync.dma_start(out=gate[1][:], in_=wgt[:, EARLY:])
         nc.sync.dma_start(out=bias[:], in_=b.rearrange("(p t) -> p t", t=PACK))
 
-        warm = sbuf([P, 1], F32, "warm")
-        nc.vector.memset(warm[:], 0.0)
-        warm_out = sbuf([P, 1], F32, "warm_out")
-        nc.scalar.activation(out=warm_out[:], in_=warm[:], func=SILU)
-
         ones = sbuf([P, P], F32, "ones")
         nc.vector.memset(ones[:], 1.0)
+        warm_out = sbuf([P, 1], F32, "warm_out")
+        nc.scalar.activation(out=warm_out[:], in_=ones[:, 0:1], func=SILU)
+        eye_in = reuse.tile([P, 2 * K + 4], BF16, name="eye_in", offset=0, align_bytes=64)
+        nc.vector.memset(eye_in[:].bitcast(I32), 0)
+        column = sbuf([P, P], F32, "column")
+        nc.vector.tensor_tensor_scan(out=column[:], data0=ones[:], data1=ones[:], initial=0.0, op0=MULT, op1=ADD)
         quadrant = sbuf([P, 1], F32, "quadrant")
         for first in range(0, P, 32):
             nc.vector.memset(quadrant[first : first + 32, :], -float(first))
-        column = sbuf([P, P], F32, "column")
-        nc.vector.tensor_tensor_scan(out=column[:], data0=ones[:], data1=ones[:], initial=0.0, op0=MULT, op1=ADD)
         row = sbuf([P, 32], F32, "row")
         nc.vector.transpose(out=row[:], in_=column[:, :32])
-        eye_in = reuse.tile([P, 2 * K + 4], BF16, name="eye_in", offset=0, align_bytes=64)
-        nc.vector.memset(eye_in[:].bitcast(I32), 0)
         eye_high = sbuf([P, 2 * P + 1], U32, "eye_high")
         eye_low = sbuf([P, 2 * P], U32, "eye_low")
         eye_scales = sbuf([P, 2 * P], U8, "eye_scales")
         plain_scales = sbuf([P, N], U8, "plain_scales")
         nc.vector.memset(eye_high[:, 2 * P :], 0)
-        nc.vector.memset(plain_scales[:].bitcast(I32), 0)
         eye_ones = eye_in[:, 2:].rearrange("p (r x) -> p r x", r=2)[:, :, 0:K:PACK]
         nc.vector.tensor_scalar(out=eye_ones, in0=column[:].unsqueeze(1).to_broadcast([P, 2, P]), scalar1=quadrant[:], scalar2=row[:, 0:1],
                                 op0=ADD, op1=EQUAL)
+        nc.vector.memset(plain_scales[:].bitcast(I32), 0)
         nc.vector.quantize_mx(out=eye_high[:, : 2 * P].bitcast(FP8X4), scales=eye_scales[:], in_=eye_in[:, : 2 * K])
         nc.scalar.copy(out=eye_low[:].bitcast(U16), in_=eye_high[:].bitcast(U16)[:, 1 : 4 * P + 1])
 

@@ -46,7 +46,8 @@ def tile_list_tier_no_siluP_kernel(tc, xT, wgt, wt, b, offs, out_0, out_1, out_2
         offsets = lists.tile([P, J // 16], U16, name="offsets")
         x_rows = xT.rearrange("(p i) t -> p i t", i=PACK)
         picks = sbuf([P, PACK * EARLY], F32, "picks")
-        w_raw = (sbuf([P, PACK, 2 * P], F32, "w_raw")[:], picks[:, EARLY - P : EARLY - P + 2 * N].rearrange("p (i n) -> p i n", i=PACK))
+        lows = [reuse.tile([P, 2, EARLY // 2], F32, name="low%d" % h, offset=4096 + h * 4 * EARLY, align_bytes=64) for h in range(2)]
+        w_raw = (sbuf([P, PACK, 2 * P], F32, "w_raw")[:], reuse.tile([P, PACK, 2 * P], F32, name="w_raw1", offset=4096, align_bytes=64)[:])
         x_plane = [sbuf([P, T], F32, "x_plane%d" % i) for i in range(PACK)]
         gate = [sbuf([P, width], F32, "gate%d" % width) for width in (EARLY, J - EARLY)]
         bias = sbuf([P, PACK], F32, "bias")
@@ -126,13 +127,12 @@ def tile_list_tier_no_siluP_kernel(tc, xT, wgt, wt, b, offs, out_0, out_1, out_2
         subtract_w(1)
         subtract_w(2)
         main_codes = sbuf([P, N], U32, "main_codes")
-        main_scales = sbuf([P, N], U8, "main_scales")
+        main_scales = reuse.tile([P, N], U8, name="main_scales", offset=4096 + 4 * EARLY + 2048, align_bytes=64)
 
         def deal(dealt, by_quarter):
             nc.scalar.copy(out=dealt.rearrange("p (t h m) -> p h t m", t=PACK, h=2), in_=by_quarter.rearrange("p (h t m) -> p h t m", t=PACK, h=2))
 
         deal(main_codes[:], plain_codes[:])
-        deal(main_scales[:].bitcast(U32), plain_scales[:].bitcast(U32))
         subtract_w(3)
 
         rest_codes = sbuf([P, N], U32, "rest_codes")
@@ -144,6 +144,8 @@ def tile_list_tier_no_siluP_kernel(tc, xT, wgt, wt, b, offs, out_0, out_1, out_2
 
         def gather(i, j0, width):
             dst, weights = (picked[:, i, j0 : j0 + width], gate[0][:, j0 : j0 + width]) if j0 < EARLY else (late[:, i // 2, i % 2], gate[1][:])
+            if i < 2 and j0 < EARLY:
+                dst = lows[2 * j0 // EARLY][:, i]
             nc.vector.tensor_tensor(out=dst, in0=x_plane[i][:].indirect(offsets[:, j0 // 16 : (j0 + width) // 16]), in1=weights, op=MULT)
 
         def quantise_rest(u):
@@ -152,7 +154,8 @@ def tile_list_tier_no_siluP_kernel(tc, xT, wgt, wt, b, offs, out_0, out_1, out_2
 
         quantise_rest(0)
         quantise_rest(1)
-        gather(0, 0, EARLY)
+        gather(0, 0, EARLY // 2)
+        gather(0, EARLY // 2, EARLY // 2)
         gather(1, 0, EARLY // 2)
         gather(1, EARLY // 2, EARLY // 2)
         gather(2, 0, EARLY)
@@ -182,11 +185,18 @@ def tile_list_tier_no_siluP_kernel(tc, xT, wgt, wt, b, offs, out_0, out_1, out_2
 
         low, high = slice(0, 2), slice(2, 4)
         for c in range(LATE):
-            weave_x(c, nc.scalar, 0, CHUNKS[c], low)
+            first = starts[c] % (EARLY // 2)
+            weave(nc.scalar, xg[c].rearrange("p (j i) -> p j i", i=PACK)[:, :, low], lows[c // 2][:, :, first : first + CHUNKS[c]], None)
+        deal(main_scales[:].bitcast(U32), plain_scales[:].bitcast(U32))
+        for half in range(2):
+            idle = psum.tile([P, N], F32, name="idle", tag="bank")
+            part = slice(half * P, (half + 1) * P)
+            nc.tensor.matmul_mx(out=idle[:], lhsT=eye_high[:, part].bitcast(FP8X4), lhsT_scale=eye_scales[:, part],
+                                rhs=main_codes[:].bitcast(FP8X4), rhs_scale=main_scales[:], start=True, stop=True)
 
         def quantise_x(c):
             w = CHUNKS[c]
-            codes = sbuf([P, w], U32, "xg_codes%d" % c)
+            codes = reuse.tile([P, w], U32, name="xg_codes2", offset=0, align_bytes=64) if c == 2 else sbuf([P, w], U32, "xg_codes%d" % c)
             scales = sbuf([P, w], U8, "xg_scales%d" % c)
             nc.vector.quantize_mx(out=codes[:].bitcast(FP8X4), scales=scales[:], in_=xg[c])
             xq[c] = (codes, scales)
@@ -211,7 +221,7 @@ def tile_list_tier_no_siluP_kernel(tc, xT, wgt, wt, b, offs, out_0, out_1, out_2
 
         y_codes = [sbuf([P, hi - lo], U32, "y_codes%d" % lo) for lo, hi in STORE_GROUPS]
         grouped = {c: sbuf([P, CHUNKS[c], PACK], BF16, "y_grouped%d" % c)[:] for c in (0, 2, 3)}
-        grouped[1] = picks[:, 2 * EARLY + starts[1] : 2 * EARLY + starts[1] + 2 * CHUNKS[1]].bitcast(BF16).rearrange("p (j i) -> p j i", i=PACK)
+        grouped[1] = reuse.tile([P, CHUNKS[1], PACK], BF16, name="y_grouped1", offset=0, align_bytes=64)[:]
 
         def weave_y(c, engine, lo=0, hi=None):
             share = (lo, hi or CHUNKS[c])
@@ -242,6 +252,7 @@ def tile_list_tier_no_siluP_kernel(tc, xT, wgt, wt, b, offs, out_0, out_1, out_2
         weave_x(2, nc.vector, 256, 384, high)
         quantise_x(2)
         multiply(2)
+        weave_y(1, nc.scalar, 128, 256)
         for i in range(PACK):
             gather(i, EARLY, 256)
         weave_y(0, nc.vector)
@@ -249,7 +260,7 @@ def tile_list_tier_no_siluP_kernel(tc, xT, wgt, wt, b, offs, out_0, out_1, out_2
         quantise_y(0)
         quantise_x(3)
         multiply(3)
-        weave_y(1, nc.vector)
+        weave_y(1, nc.vector, 0, 128)
         quantise_y(1)
         store_words(0)
         weave_y(2, nc.vector, 0, 256)

@@ -61,19 +61,20 @@ def tile_list_tier_no_siluP_kernel(tc, xT, wgt, wt, b, offs, out_0, out_1, out_2
         nc.sync.dma_start(out=gate[1][:], in_=wgt[:, EARLY:])
         nc.sync.dma_start(out=bias[:], in_=b.rearrange("(p t) -> p t", t=PACK))
 
-        ones = sbuf([P, P], F32, "ones")
+        ones = sbuf([P, 1], F32, "ones")
         nc.vector.memset(ones[:], 1.0)
         warm_out = sbuf([P, 1], F32, "warm_out")
-        nc.scalar.activation(out=warm_out[:], in_=ones[:, 0:1], func=SILU)
-        eye_in = reuse.tile([P, 2 * K + 4], BF16, name="eye_in", offset=0, align_bytes=64)
-        nc.vector.memset(eye_in[:].bitcast(I32), 0)
+        nc.scalar.activation(out=warm_out[:], in_=ones[:], func=SILU)
+        eye_in = sbuf([P, 2 * K + 4], BF16, "eye_in")
+        nc.vector.memset(eye_in[:, :K].bitcast(I32), 0)
         column = sbuf([P, P], F32, "column")
-        nc.vector.tensor_tensor_scan(out=column[:], data0=ones[:], data1=ones[:], initial=0.0, op0=MULT, op1=ADD)
+        nc.vector.tensor_tensor_scan(out=column[:], data0=ones[:].to_broadcast([P, P]), data1=ones[:].to_broadcast([P, P]), initial=0.0, op0=MULT, op1=ADD)
         quadrant = sbuf([P, 1], F32, "quadrant")
         for first in range(0, P, 32):
             nc.vector.memset(quadrant[first : first + 32, :], -float(first))
         row = sbuf([P, 32], F32, "row")
         nc.vector.transpose(out=row[:], in_=column[:, :32])
+        nc.vector.memset(eye_in[:, K:].bitcast(I32), 0)
         eye_high = sbuf([P, 2 * P + 1], U32, "eye_high")
         eye_low = sbuf([P, 2 * P], U32, "eye_low")
         eye_scales = sbuf([P, 2 * P], U8, "eye_scales")
@@ -266,10 +267,10 @@ def tile_list_tier_no_siluP_kernel(tc, xT, wgt, wt, b, offs, out_0, out_1, out_2
         weave_y(2, nc.vector, 0, 256)
         weave_y(2, nc.vector, 256, 384)
         quantise_y(2, 0, 256)
-        weave_y(3, nc.scalar, 160, 256)
-        weave_y(3, nc.vector, 0, 160)
         quantise_y(2, 256, 384)
         store_words(1)
+        weave_y(3, nc.scalar, 160, 256)
+        weave_y(3, nc.vector, 0, 160)
         quantise_y(3)
         store_words(2)
         for quad in range(4):

@@ -140,13 +140,16 @@ def tile_list_tier_no_siluP_kernel(tc, xT, wgt, wt, b, offs, out_0, out_1, out_2
         rest_scales = sbuf([P, N], U8, "rest_scales")
         tiers = ((main_codes, main_scales), (rest_codes, rest_scales))
 
-        picked = picks[:].rearrange("p (i j) -> p i j", i=PACK)
-        late = picked[:, 2:, starts[1] : starts[1] + 2 * CHUNKS[LATE]].rearrange("p a (b j) -> p b a j", b=2)
+        highs = picks[:, : 2 * EARLY].rearrange("p (h a j) -> p h a j", h=2, a=2)
+        late = picks[:, : 2 * EARLY].rearrange("p (i j) -> p i j", i=PACK)[:, :, P:]
 
         def gather(i, j0, width):
-            dst, weights = (picked[:, i, j0 : j0 + width], gate[0][:, j0 : j0 + width]) if j0 < EARLY else (late[:, i // 2, i % 2], gate[1][:])
-            if i < 2 and j0 < EARLY:
-                dst = lows[2 * j0 // EARLY][:, i]
+            h, first = divmod(j0, EARLY // 2)
+            if j0 >= EARLY:
+                dst = late[:, i]
+            else:
+                dst = (lows[h][:, i] if i < 2 else highs[:, h, i - 2])[:, first : first + width]
+            weights = gate[0][:, j0 : j0 + width] if j0 < EARLY else gate[1][:]
             nc.vector.tensor_tensor(out=dst, in0=x_plane[i][:].indirect(offsets[:, j0 // 16 : (j0 + width) // 16]), in1=weights, op=MULT)
 
         def quantise_rest(u):
@@ -159,7 +162,8 @@ def tile_list_tier_no_siluP_kernel(tc, xT, wgt, wt, b, offs, out_0, out_1, out_2
         gather(0, EARLY // 2, EARLY // 2)
         gather(1, 0, EARLY // 2)
         gather(1, EARLY // 2, EARLY // 2)
-        gather(2, 0, EARLY)
+        gather(2, 0, EARLY // 2)
+        gather(2, EARLY // 2, EARLY // 2)
 
         out_rows = out_0.rearrange("(p t) j -> p t j", t=PACK)
         out_words = out_1.rearrange("a p j i -> p (a j i)").bitcast(I32)
@@ -179,10 +183,11 @@ def tile_list_tier_no_siluP_kernel(tc, xT, wgt, wt, b, offs, out_0, out_1, out_2
 
         def weave_x(c, engine, lo, hi, planes):
             dst = xg[c].rearrange("p (j i) -> p j i", i=PACK)[:, :, planes]
-            weave(engine, dst, picked[:, planes, starts[c] : starts[c] + CHUNKS[c]], ((lo, hi), (lo, hi)))
+            first = starts[c] % (EARLY // 2)
+            weave(engine, dst, highs[:, c // 2, :, first : first + CHUNKS[c]], ((lo, hi), (lo, hi)))
 
         def weave_late():
-            nc.vector.tensor_copy(out=xg[LATE].rearrange("p (c e b a) -> p c b a e", e=2, b=2, a=2), in_=late.rearrange("p b a (c e) -> p c b a e", e=2))
+            weave(nc.vector, xg[LATE].rearrange("p (j i) -> p j i", i=PACK), late, None)
 
         low, high = slice(0, 2), slice(2, 4)
         for c in range(LATE):
@@ -243,18 +248,18 @@ def tile_list_tier_no_siluP_kernel(tc, xT, wgt, wt, b, offs, out_0, out_1, out_2
         weave_x(0, nc.scalar, 0, 128, high)
         gather(3, 128, 256)
         weave_x(1, nc.scalar, 0, 256, high)
-        gather(3, 384, 256)
-        weave_x(2, nc.scalar, 0, 256, high)
+        gather(3, 384, 384)
+        weave_x(2, nc.scalar, 0, 384, high)
         quantise_x(0)
         multiply(0)
-        gather(3, 640, 128)
         quantise_x(1)
         multiply(1)
-        weave_x(2, nc.vector, 256, 384, high)
+        gather(0, EARLY, 256)
+        gather(1, EARLY, 256)
         quantise_x(2)
         multiply(2)
         weave_y(1, nc.scalar, 128, 256)
-        for i in range(PACK):
+        for i in range(2, PACK):
             gather(i, EARLY, 256)
         weave_y(0, nc.vector)
         weave_late()

from contextlib import ExitStack

import concourse.mybir as mybir

K, N, T, J = 512, 512, 2048, 1024
FLOPS = 2 * 2 * K * N * J + 2 * K * K * N

F32 = mybir.dt.float32
BF16 = mybir.dt.bfloat16
I32 = mybir.dt.int32
U32 = mybir.dt.uint32
U16 = mybir.dt.uint16
U8 = mybir.dt.uint8
FP8X4 = mybir.dt.float8_e4m3fn_x4
MULT = mybir.AluOpType.mult
ADD = mybir.AluOpType.add
EQUAL = mybir.AluOpType.is_equal
SUBTRACT = mybir.AluOpType.subtract
SILU = mybir.ActivationFunctionType.Silu

P = 128
PACK = 4
CHUNKS = (128, 256, 384, 256)
EARLY = 768
LATE = 3
STORE_GROUPS = ((0, 384), (384, 768), (768, 1024))


def tile_list_tier_no_siluP_kernel(tc, xT, wgt, wt, b, offs, out_0, out_1, out_2):
    nc = tc.nc
    with ExitStack() as ctx:
        lists = ctx.enter_context(tc.tile_pool(name="lists", bufs=1))
        keep = ctx.enter_context(tc.tile_pool(name="keep", bufs=1))
        reuse = ctx.enter_context(tc.tile_pool(name="reuse", bufs=1))
        psum = ctx.enter_context(tc.psum_pool(name="psum", bufs=8))

        def sbuf(shape, dtype, name):
            return keep.tile(shape, dtype, name=name, align_bytes=64)

        def pairs(ap, layout):
            return ap.rearrange("p %s -> p c i e" % layout, e=2)


        starts = [sum(CHUNKS[:c]) for c in range(len(CHUNKS))]

        offsets = lists.tile([P, J // 16], U16, name="offsets")
        x_rows = xT.rearrange("(p i) t -> p i t", i=PACK)
        picks = sbuf([P, PACK * EARLY], F32, "picks")
        lows = [reuse.tile([P, 2, EARLY // 2], F32, name="low%d" % h, offset=4096 + h * 4 * EARLY, align_bytes=64) for h in range(2)]
        w_raw = (sbuf([P, PACK, 2 * P], F32, "w_raw")[:], reuse.tile([P, PACK, 2 * P], F32, name="w_raw1", offset=4096, align_bytes=64)[:])
        x_plane = [sbuf([P, T], F32, "x_plane%d" % i) for i in range(PACK)]
        gate = [sbuf([P, width], F32, "gate%d" % width) for width in (EARLY, J - EARLY)]
        bias = sbuf([P, PACK], F32, "bias")
        for h in range(2):
            nc.sync.dma_start(out=w_raw[h], in_=wt.rearrange("(p i) n -> p i n", i=PACK)[:, :, h * 2 * P : (h + 1) * 2 * P])
        nc.sync.dma_start(offsets[:], offs)
        nc.sync.dma_start(out=x_plane[0][:], in_=x_rows[:, 0, :])
        nc.sync.dma_start(out=gate[0][:], in_=wgt[:, :EARLY])
        for i in range(1, PACK):
            nc.sync.dma_start(out=x_plane[i][:], in_=x_rows[:, i, :])
        nc.sync.dma_start(out=gate[1][:], in_=wgt[:, EARLY:])
        nc.sync.dma_start(out=bias[:], in_=b.rearrange("(p t) -> p t", t=PACK))

        ones = sbuf([P, 1], F32, "ones")
        nc.vector.memset(ones[:], 1.0)
        warm_out = sbuf([P, 1], F32, "warm_out")
        nc.scalar.activation(out=warm_out[:], in_=ones[:], func=SILU)
        eye_in = sbuf([P, 2 * K + 4], BF16, "eye_in")
        nc.vector.memset(eye_in[:, :K].bitcast(I32), 0)
        column = sbuf([P, P], F32, "column")
        nc.vector.tensor_tensor_scan(out=column[:], data0=ones[:].to_broadcast([P, P]), data1=ones[:].to_broadcast([P, P]), initial=0.0, op0=MULT, op1=ADD)
        quadrant = sbuf([P, 1], F32, "quadrant")
        for first in range(0, P, 32):
            nc.vector.memset(quadrant[first : first + 32, :], -float(first))
        row = sbuf([P, 32], F32, "row")
        nc.vector.transpose(out=row[:], in_=column[:, :32])
        nc.vector.memset(eye_in[:, K:].bitcast(I32), 0)
        eye_high = sbuf([P, 2 * P + 1], U32, "eye_high")
        eye_low = sbuf([P, 2 * P], U32, "eye_low")
        eye_scales = sbuf([P, 2 * P], U8, "eye_scales")
        plain_scales = sbuf([P, N], U8, "plain_scales")
        nc.vector.memset(eye_high[:, 2 * P :], 0)
        eye_ones = eye_in[:, 2:].rearrange("p (r x) -> p r x", r=2)[:, :, 0:K:PACK]
        nc.vector.tensor_scalar(out=eye_ones, in0=column[:].unsqueeze(1).to_broadcast([P, 2, P]), scalar1=quadrant[:], scalar2=row[:, 0:1],
                                op0=ADD, op1=EQUAL)
        nc.vector.memset(plain_scales[:].bitcast(I32), 0)
        nc.vector.quantize_mx(out=eye_high[:, : 2 * P].bitcast(FP8X4), scales=eye_scales[:], in_=eye_in[:, : 2 * K])
        nc.scalar.copy(out=eye_low[:].bitcast(U16), in_=eye_high[:].bitcast(U16)[:, 1 : 4 * P + 1])

        plain = reuse.tile([P, 3 * K], BF16, name="plain", offset=0, align_bytes=64)
        rounded = [plain[:, slot * K : (slot + 1) * K] for slot in (0, 1, 1, 2)]
        plain_codes = sbuf([P, N], U32, "plain_codes")
        raws = [w_raw[q // 2].rearrange("p i (m u e) -> p u m i e", u=2, e=2)[:, q % 2] for q in range(4)]
        rest_dealt = (picks[:, 3 * EARLY + 160 : 3 * EARLY + 160 + N].bitcast(BF16),
                      sbuf([P, 2 * N], BF16, "rest_dealt")[:])
        rest_slots = [half.rearrange("p (e m i) -> p m i e", e=2, i=PACK) for half in rest_dealt]
        values = {}

        def round_w(q):
            copy = nc.vector.tensor_copy if q % 2 == 0 else nc.scalar.copy
            copy(out=rounded[q].rearrange("p (e m i) -> p m i e", e=2, i=PACK), in_=raws[q])

        def quantise_w(q):
            cols = slice(q * P, (q + 1) * P)
            nc.vector.quantize_mx(out=plain_codes[:, cols].bitcast(FP8X4), scales=plain_scales[:, cols], in_=rounded[q])
            values[q] = psum.tile([P, PACK, P], F32, name="values", tag="bank")
            for i in (2, 3, 0, 1):
                eye_codes = eye_high if i >= 2 else eye_low
                part = slice((i % 2) * P, (i % 2 + 1) * P)
                nc.tensor.matmul_mx(out=values[q][:, i, :], lhsT=eye_codes[:, part].bitcast(FP8X4), lhsT_scale=eye_scales[:, part],
                                    rhs=plain_codes[:, cols].bitcast(FP8X4), rhs_scale=plain_scales[:, cols], start=True, stop=True)

        def subtract_w(q):
            step = 32 if q == 0 else 64
            for lo in range(0, 64, step):
                nc.vector.tensor_tensor(out=rest_slots[q % 2][:, 64 * (q // 2) + lo : 64 * (q // 2) + lo + step], in0=raws[q][:, lo : lo + step],
                                        in1=values[q][:].rearrange("p i (e m) -> p m i e", e=2)[:, lo : lo + step], op=SUBTRACT)

        round_w(0)
        round_w(1)
        round_w(3)
        quantise_w(0)
        quantise_w(1)
        round_w(2)
        subtract_w(0)
        quantise_w(2)
        quantise_w(3)
        subtract_w(1)
        subtract_w(2)
        main_codes = sbuf([P, N], U32, "main_codes")
        main_scales = reuse.tile([P, N], U8, name="main_scales", offset=4096 + 4 * EARLY + 2048, align_bytes=64)

        def deal(dealt, by_quarter):
            nc.scalar.copy(out=dealt.rearrange("p (t h m) -> p h t m", t=PACK, h=2), in_=by_quarter.rearrange("p (h t m) -> p h t m", t=PACK, h=2))

        deal(main_codes[:], plain_codes[:])
        subtract_w(3)

        rest_codes = sbuf([P, N], U32, "rest_codes")
        rest_scales = sbuf([P, N], U8, "rest_scales")
        tiers = ((main_codes, main_scales), (rest_codes, rest_scales))

        highs = picks[:, : 2 * EARLY].rearrange("p (h a j) -> p h a j", h=2, a=2)
        late = picks[:, : 2 * EARLY].rearrange("p (i j) -> p i j", i=PACK)[:, :, P:]

        def gather(i, j0, width):
            h, first = divmod(j0, EARLY // 2)
            if j0 >= EARLY:
                dst = late[:, i]
            else:
                dst = (lows[h][:, i] if i < 2 else highs[:, h, i - 2])[:, first : first + width]
            weights = gate[0][:, j0 : j0 + width] if j0 < EARLY else gate[1][:]
            nc.vector.tensor_tensor(out=dst, in0=x_plane[i][:].indirect(offsets[:, j0 // 16 : (j0 + width) // 16]), in1=weights, op=MULT)

        def quantise_rest(u):
            cols = slice(u * 2 * P, (u + 1) * 2 * P)
            nc.vector.quantize_mx(out=rest_codes[:, cols].bitcast(FP8X4), scales=rest_scales[:, cols], in_=rest_dealt[u])

        quantise_rest(0)
        quantise_rest(1)
        gather(0, 0, EARLY // 2)
        gather(0, EARLY // 2, EARLY // 2)
        gather(1, 0, EARLY // 2)
        gather(1, EARLY // 2, EARLY // 2)
        gather(2, 0, EARLY // 2)
        gather(2, EARLY // 2, EARLY // 2)

        out_rows = out_0.rearrange("(p t) j -> p t j", t=PACK)
        out_words = out_1.rearrange("a p j i -> p (a j i)").bitcast(I32)
        out_scales = out_2.rearrange("a q j -> (a q) j").bitcast(I32)
        y_scales = sbuf([P, J], U8, "y_scales")
        xg = {}
        xq = {}
        ys = {}

        def weave(engine, dst, src, shares):
            lo, hi = (0, src.shape[2]) if shares is None else shares[1 if engine is nc.vector else 0]
            copy = nc.vector.tensor_copy if engine is nc.vector else nc.scalar.copy
            copy(out=pairs(dst[:, lo:hi], "(c e) i"), in_=pairs(src[:, :, lo:hi], "i (c e)"))

        for c, w in enumerate(CHUNKS):
            xg[c] = sbuf([P, w * PACK], BF16, "xg%d" % c)[:]

        def weave_x(c, engine, lo, hi, planes):
            dst = xg[c].rearrange("p (j i) -> p j i", i=PACK)[:, :, planes]
            first = starts[c] % (EARLY // 2)
            weave(engine, dst, highs[:, c // 2, :, first : first + CHUNKS[c]], ((lo, hi), (lo, hi)))

        def weave_late():
            weave(nc.vector, xg[LATE].rearrange("p (j i) -> p j i", i=PACK), late, None)

        low, high = slice(0, 2), slice(2, 4)
        for c in range(LATE):
            first = starts[c] % (EARLY // 2)
            weave(nc.scalar, xg[c].rearrange("p (j i) -> p j i", i=PACK)[:, :, low], lows[c // 2][:, :, first : first + CHUNKS[c]], None)
        deal(main_scales[:].bitcast(U32), plain_scales[:].bitcast(U32))
        for half in range(2):
            idle = psum.tile([P, N], F32, name="idle", tag="bank")
            part = slice(half * P, (half + 1) * P)
            nc.tensor.matmul_mx(out=idle[:], lhsT=eye_high[:, part].bitcast(FP8X4), lhsT_scale=eye_scales[:, part],
                                rhs=main_codes[:].bitcast(FP8X4), rhs_scale=main_scales[:], start=True, stop=True)

        def quantise_x(c):
            w = CHUNKS[c]
            codes = reuse.tile([P, w], U32, name="xg_codes2", offset=0, align_bytes=64) if c == 2 else sbuf([P, w], U32, "xg_codes%d" % c)
            scales = sbuf([P, w], U8, "xg_scales%d" % c)
            nc.vector.quantize_mx(out=codes[:].bitcast(FP8X4), scales=scales[:], in_=xg[c])
            xq[c] = (codes, scales)

        def multiply(c):
            w = CHUNKS[c]
            codes, scales = xq[c]
            y = sbuf([P, PACK, w], F32, "y%d" % c)
            ys[c] = y
            for t in range(PACK):
                acc = psum.tile([P, w], F32, name="acc", tag="bank")
                for lo in range(0, w, 256):
                    cols = slice(lo, min(lo + 256, w))
                    for n, (w_codes, w_scales) in enumerate(tiers):
                        nc.tensor.matmul_mx(out=acc[:, cols], lhsT=w_codes[:, t * P : (t + 1) * P].bitcast(FP8X4),
                                            lhsT_scale=w_scales[:, t * P : (t + 1) * P],
                                            rhs=codes[:, cols].bitcast(FP8X4), rhs_scale=scales[:, cols], start=(n == 0), stop=(n == 1))
                nc.scalar.activation(out=y[:, t, :], in_=acc[:], func=SILU, bias=bias[:, t : t + 1])
                rows = 4 if w == 128 else 2
                if (t + 1) % rows == 0:
                    nc.sync.dma_start(out=out_rows[:, t + 1 - rows : t + 1, starts[c] : starts[c] + w], in_=y[:, t + 1 - rows : t + 1, :])

        y_codes = [sbuf([P, hi - lo], U32, "y_codes%d" % lo) for lo, hi in STORE_GROUPS]
        grouped = {c: sbuf([P, CHUNKS[c], PACK], BF16, "y_grouped%d" % c)[:] for c in (0, 2, 3)}
        grouped[1] = reuse.tile([P, CHUNKS[1], PACK], BF16, name="y_grouped1", offset=0, align_bytes=64)[:]

        def weave_y(c, engine, lo=0, hi=None):
            share = (lo, hi or CHUNKS[c])
            weave(engine, grouped[c], ys[c][:], (share, share))

        def quantise_y(c, lo=0, hi=None):
            hi = hi or CHUNKS[c]
            g = max(c - 1, 0)
            first = starts[c] - STORE_GROUPS[g][0]
            nc.vector.quantize_mx(out=y_codes[g][:, first + lo : first + hi].bitcast(FP8X4), scales=y_scales[:, starts[c] + lo : starts[c] + hi],
                                  in_=grouped[c][:, lo:hi].rearrange("p j t -> p (j t)"))

        def store_words(g):
            lo, hi = STORE_GROUPS[g]
            nc.sync.dma_start(out=out_words[:, lo:hi], in_=y_codes[g][:].bitcast(I32))

        gather(3, 0, 128)
        weave_x(0, nc.scalar, 0, 128, high)
        gather(3, 128, 256)
        weave_x(1, nc.scalar, 0, 256, high)
        gather(3, 384, 384)
        weave_x(2, nc.scalar, 0, 384, high)
        quantise_x(0)
        multiply(0)
        quantise_x(1)
        multiply(1)
        gather(0, EARLY, 256)
        gather(1, EARLY, 256)
        quantise_x(2)
        multiply(2)
        weave_y(1, nc.scalar, 128, 256)
        for i in range(2, PACK):
            gather(i, EARLY, 256)
        weave_y(0, nc.vector)
        weave_late()
        quantise_y(0)
        quantise_x(3)
        multiply(3)
        weave_y(1, nc.vector, 0, 128)
        quantise_y(1)
        store_words(0)
        weave_y(2, nc.vector, 0, 256)
        weave_y(2, nc.vector, 256, 384)
        quantise_y(2, 0, 256)
        quantise_y(2, 256, 384)
        store_words(1)
        weave_y(3, nc.scalar, 160, 256)
        weave_y(3, nc.vector, 0, 160)
        quantise_y(3)
        store_words(2)
        for quad in range(4):
            queue = nc.sync if quad % 2 == 0 else nc.scalar
            queue.dma_start(out=out_scales[4 * quad : 4 * quad + 4, :],
                            in_=y_scales[32 * quad : 32 * quad + 4, :].bitcast(I32))
